import numpy as np, ml_dtypes
CORES = [36,164,52,180,100,228,116,244]
N = 8
BF = ml_dtypes.bfloat16
def gentries(a):
    return np.ascontiguousarray(a.reshape(8, 16, -1).transpose(0, 2, 1)).reshape(8, -1)
def gtable(e):
    e = np.asarray(e); return np.ascontiguousarray(e.reshape(8, -1, 16).transpose(0, 2, 1)).reshape(128, -1).astype(np.int32)
def f(rng, *shape):
    return (rng.standard_normal(shape, dtype=np.float32) * np.exp2(rng.integers(-2, 3, shape[:-1] + (1,)))).astype(BF)
def wide(rng, *shape):
    v = f(rng, *shape).astype(np.float32); k = shape[:-2] + (1, shape[-1])
    return (v * np.exp2(rng.integers(-6, 7, k)) * (rng.random(k) > 0.0625)).astype(BF)
R, G, NT, E, RD = 1024, 128, 256, 3, 4
H, W = R // 2, R + N * G
def energies(rng, n):
    v = rng.standard_normal((N, 8, 16, n), dtype=np.float32) * np.exp2(rng.integers(-1, 2, (N, 8, 1, 1))).astype(np.float32)
    return v.reshape(N, 128, n).astype(BF)
def glist(e):
    return np.stack([gtable(v) for v in e])
def ungl(a):
    return np.stack([gentries(v) for v in a]).astype(np.int64)
def setup_inputs(rng):
    return {"own": energies(rng, R), "pair": energies(rng, 16 * NT), "st": rng.integers(0, 16, (N, 8, R)).astype(np.int32),
            "nb": glist(rng.integers(0, W, (N, 8, E * R))), "th": glist(rng.integers(0, W, (N, 8, E * R))), "tb": glist(rng.integers(0, NT, (N, 8, E * R))),
            "sd": glist(rng.integers(0, R, (N, 8, N * G)))}
def setup_inputs_ties(rng):
    d = setup_inputs(rng)
    own = rng.integers(0, 2, (N, 128, R)).astype(np.float32); pair = rng.integers(0, 3, (N, 128, 16 * NT)).astype(np.float32)
    q, g = int(rng.integers(0, N)), int(rng.integers(0, 8)); own[q, 16 * g:16 * g + 16] = 0; pair[q, 16 * g:16 * g + 16] = 0
    d["own"] = own.astype(BF); d["pair"] = pair.astype(BF); return d
def setup_inputs_ends(rng):
    d = setup_inputs(rng); v = np.array([0, H - 1, H, R - 1, R, R + G - 1, R + G, W - G, W - 1])
    d["nb"] = glist(rng.choice(v, (N, 8, E * R))); d["th"] = glist(rng.choice(v, (N, 8, E * R)))
    d["tb"] = glist(rng.choice(np.array([0, 1, NT - 2, NT - 1]), (N, 8, E * R))); d["sd"] = glist(rng.choice(np.array([0, H - 1, H, R - 1]), (N, 8, N * G)))
    d["st"] = rng.choice(np.array([0, 15]), (N, 8, R)).astype(np.int32)
    o = d["own"].astype(np.float32).reshape(N, 8, 16, R); o[:, :, 1:15] += 96; d["own"] = o.reshape(N, 128, R).astype(BF); return d
def setup_inputs_far(rng):
    d = setup_inputs(rng); q = (np.arange(N)[:, None, None] + 1 + np.arange(8)[None, :, None] % (N - 1)) % N
    m = np.tile(np.arange(E * R) % G, (N, 8, 1))
    d["nb"] = glist(R + G * q + rng.permuted(m, axis=2)); d["th"] = glist(R + G * q + rng.permuted(m, axis=2))
    d["sd"] = glist(rng.permuted(np.tile(np.arange(R), (N, 8, N, 1)), axis=3)[..., :G].reshape(N, 8, N * G))
    big = rng.random((N, 8, 1, 1)) < 0.5; b, g = int(rng.integers(0, N)), int(rng.integers(0, 8)); big[b, g] = True
    z = np.where(big, 2.0 ** 32, 1.0).astype(np.float32)
    o = d["own"].astype(np.float32).reshape(N, 8, 16, R); o[b, g] = np.abs(o[b, g]) + 64
    d["own"] = (o * z).reshape(N, 128, R).astype(BF)
    d["pair"] = (d["pair"].astype(np.float32).reshape(N, 8, 16, 16 * NT) * z).reshape(N, 128, 16 * NT).astype(BF); return d
def setup_inputs_alike(rng):
    d = setup_inputs(rng)
    for k, top in (("nb", W), ("th", W), ("tb", NT)):
        d[k] = glist(np.repeat(rng.integers(0, top, (N, 8, 2 * E)), H, axis=2))
    d["sd"] = glist(np.repeat(rng.integers(0, R, (N, 8, N)), G, axis=2))
    d["pair"] = (d["pair"].astype(np.float32) * np.float32(0.25)).astype(BF); return d
def setup_inputs_spread(rng):
    d = setup_inputs(rng); d["own"] = wide(rng, N, 128, R); d["pair"] = wide(rng, N, 128, 16 * NT); return d
def check_inputs(d):
    bad = []
    for k, top in (("nb", W), ("th", W), ("tb", NT), ("sd", R), ("st", 16)):
        if np.min(d[k]) < 0 or np.max(d[k]) >= top:
            bad.append(k)
    for k in ("own", "pair"):
        v = np.abs(d[k].astype(np.float32))
        if not np.all((v == 0) | ((v >= 2.0 ** -60) & (v <= 2.0 ** 40))):
            bad.append(k)
    return bad
def reference(own, pair, st, nb, th, tb, sd):
    a = own.astype(np.float32).reshape(N, 8, 16, R); p = pair.astype(np.float32).reshape(N, 8, 16, 16 * NT)
    s = st.astype(np.int64); low = np.zeros((N, 8, R), np.float32)
    near, third, base = [ungl(v).reshape(N, 8, 2, E * H) for v in (nb, th, tb)]; listed = ungl(sd)
    for t in range(RD):
        h = t & 1
        sent = np.take_along_axis(s, listed, 2).reshape(N, 8, N, G)
        w = np.concatenate([s, sent.transpose(2, 1, 0, 3).reshape(N, 8, N * G)], 2)
        col = 16 * ((base[:, :, h] + 37 * np.take_along_axis(w, third[:, :, h], 2)) & (NT - 1)) + np.take_along_axis(w, near[:, :, h], 2)
        x = np.take_along_axis(p, col[:, :, None, :], 3)
        v = a[:, :, :, h * H:(h + 1) * H]
        for k in range(E):
            v = v + x[:, :, :, k * H:(k + 1) * H]
        s[:, :, h * H:(h + 1) * H] = np.argmin(v, 2)
        low[:, :, h * H:(h + 1) * H] = np.min(v, 2)
    return {"y": s.astype(np.float32), "e": low}

@@ -1,0 +1,350 @@
+from concourse.bass import DstId, RemoteDMATransfer
+from concourse.mybir import AluOpType, ActivationFunctionType
+
+N, RD = 8, 4
+VIA_DRAM = True
+XW = 16 * 255 + 592 * 15 + 16
+MW = 264
+
+SCRATCH = {
+    "stage": ("sbuf", [128, 1024], "int32"),
+    "sdst": ("sbuf", [128, 64], "int32"),
+    "thst": ("sbuf", [128, 6, 2, 16], "int32"),
+    "nbst": ("sbuf", [128, 6, 2, 16], "int32"),
+    "tbst": ("sbuf", [128, 6, 2, 16], "int32"),
+    "osd": ("sbuf", [128, 64], "uint16"),
+    "oth": ("sbuf", [128, 192], "uint16"),
+    "onb": ("sbuf", [128, 192], "uint16"),
+    "tb16": ("sbuf", [128, 192], "bfloat16"),
+    "col": ("sbuf", [128, 96], "uint16"),
+    "win": ("sbuf", [128, 3072], "bfloat16"),
+    "snd": ("sbuf", [128, 896 * RD], "bfloat16"),
+    "owns": ("sbuf", [128, 1024], "bfloat16"),
+    "px": ("sbuf", [128, XW], "bfloat16"),
+    "zz": ("sbuf", [128, 1536], "bfloat16"),
+    "uu": ("sbuf", [128, 1536], "bfloat16"),
+    "xx": ("sbuf", [128, 1536], "bfloat16"),
+    "dif": ("sbuf", [128, 128], "float32"),
+    "idb": ("sbuf", [128, 128], "bfloat16"),
+    "idf": ("sbuf", [128, 128], "float32"),
+    "sel": ("sbuf", [128, 288], "bfloat16"),
+    "desc": ("sbuf", [128, 256], "bfloat16"),
+    "rst": ("sbuf", [128, 256], "bfloat16"),
+    "mn": ("sbuf", [128, 2 * MW], "float32"),
+    "nlt": ("sbuf", [128, 512], "bfloat16"),
+    "arg": ("sbuf", [128, 512], "bfloat16"),
+    "yo": ("sbuf", [128, 1024], "float32"),
+    "eo": ("sbuf", [128, 1024], "float32"),
+    "outd": ("dram", [7 * RD, 128, 8], "bfloat16"),
+    "land": ("dram", [8 * RD, 128, 8], "bfloat16"),
+}
+for _k in ("pc0", "pc1", "pe0", "pe1", "pb0", "pb1", "pb2", "pt"):
+    SCRATCH[_k] = ("psum", [128, 512], "float32")
+
+SEMAPHORES = (["cv", "cs", "cp", "cg", "lsd", "lst", "lth", "ltb", "lown", "lpair", "loc", "oy2", "oe2", "oy3", "oe3"]
+              + ["out%d" % t for t in range(RD)] + ["arr%d" % t for t in range(RD)] + ["inn%d" % t for t in range(RD)])
+
+
+def rank_program(g, core, T, topo):
+    r = T.rank_of(core)
+    if r is None:
+        return
+    A, F = AluOpType, ActivationFunctionType
+    V, S, P = g.vector, g.scalar, g.tensor
+    Q = {"g": g, "v": V, "s": S, "p": P, "y": g.sync}
+    known = {q: {} for q in Q}
+    cnt, clock, lastw, readers = {}, {}, {}, {}
+
+    def fix(ev):
+        return ev if ev[1] is not None else (ev[0], cnt[ev[0]])
+
+    def clk(ev):
+        return clock.get(ev) or clock.get((ev[0], None)) or {}
+
+    def need(q, evs):
+        evs = sorted(set(fix(e) for e in evs))
+        for e in evs:
+            if known[q].get(e[0], 0) >= e[1]:
+                continue
+            if any(o != e and (clk(o).get(e[0], 0) >= e[1] or (o[0] == e[0] and o[1] > e[1])) for o in evs):
+                continue
+            Q[q].wait_ge(T.sem[e[0]], e[1])
+            known[q][e[0]] = e[1]
+            for k, n in clk(e).items():
+                known[q][k] = max(known[q].get(k, 0), n)
+
+    def deps(q, rd, wr):
+        d = [lastw[x] for x in list(rd) + list(wr) if x in lastw]
+        for x in wr:
+            d += readers.get(x, [])
+        return [e for e in d if not (q == "p" and e[0] == "cp")]
+
+    def note(ev, rd, wr):
+        for x in rd:
+            readers.setdefault(x, []).append(ev)
+        for x in wr:
+            lastw[x] = ev
+            readers[x] = []
+
+    def op(q, fn, rd, wr):
+        need(q, deps(q, rd, wr))
+        sem = "c" + q
+        fn().then_inc(T.sem[sem], 1)
+        cnt[sem] = cnt.get(sem, 0) + 1
+        ev = (sem, cnt[sem])
+        clock[ev] = dict(known[q])
+        note(ev, rd, wr)
+
+    def dma(q, sem, out, in_, rd, wr):
+        need(q, deps(q, rd, wr))
+        Q[q].dma_start(out, in_).then_inc(T.sem[sem], 16)
+        cnt[sem] = cnt.get(sem, 0) + 16
+        c = clock.setdefault((sem, None), {})
+        for k, n in known[q].items():
+            c[k] = max(c.get(k, 0), n)
+        note((sem, None), rd, wr)
+
+    def gather(q, out, win, off, rd, wr):
+        if q == "v":
+            op(q, lambda: V.tensor_copy(out, win.indirect(off)), rd, wr)
+        else:
+            op(q, lambda: S.activation(out, win.indirect(off), F.Copy), rd, wr)
+
+    def flip(q, out, in_, rd, wr):
+        if q == "v":
+            op(q, lambda: V.tensor_scalar(out, in_, -1.0, 15.0, A.mult, A.add), rd, wr)
+        else:
+            op(q, lambda: S.activation(out, in_, F.Copy, bias=15.0, scale=-1.0), rd, wr)
+
+    def copy(q, out, in_, rd, wr):
+        if q == "v":
+            op(q, lambda: V.tensor_copy(out, in_), rd, wr)
+        else:
+            op(q, lambda: S.activation(out, in_, F.Copy), rd, wr)
+
+    def mms(items, rd, wr):
+        def fn():
+            last = None
+            for it in items:
+                last = P.matmul(*it)
+            return last
+        op("p", fn, rd, wr)
+
+    OWN = 0 if VIA_DRAM else 1024
+    WO = ["wa", "wb", "wc"]
+    OSD = ["osd0", "osd1"]
+
+    def rem(t):
+        return 1024 if VIA_DRAM else (2048 if t % 2 == 0 else 0)
+
+    def remn(t):
+        return "rem%d" % (0 if VIA_DRAM else t % 2)
+
+    def window(t):
+        a = 0 if (VIA_DRAM or t % 2) else 1024
+        return T.win[:, a:a + 2048]
+
+    dests = [(r + 1 + j) % N for j in range(N - 1)]
+    own_win = T.win[:, OWN:OWN + 1024]
+
+    def send(t, parts):
+        if VIA_DRAM:
+            for j in range(N - 1):
+                dma("y" if j < 4 else "s", "out%d" % t, T.outd[7 * t + j],
+                    T.snd[15::16, 896 * t + 128 * j:896 * t + 128 * j + 128], parts(j), ["od%d_%d" % (t, j)])
+            need("g", [("out%d" % t, None)])
+        else:
+            need("g", [lastw[x] for j in range(N - 1) for x in parts(j)])
+        trs = []
+        for j, d in enumerate(dests):
+            c = T.cores[d]
+            rid, pid = topo.addr(c, core)
+            if VIA_DRAM:
+                src, dst = T.outd[7 * t + j], T.land[8 * t + r]
+            else:
+                src = T.snd[:, 896 * t + 128 * j:896 * t + 128 * j + 128]
+                dst = T.win[:, rem(t) + 128 * r:rem(t) + 128 * r + 128]
+            trs.append(RemoteDMATransfer(dst_ids=[DstId(rid=rid, pnc=pid)], dma_engine_mask=1 << topo.engines(core, c)[j],
+                                         remote_sem=T.sem["arr%d" % t], src=src, dst=dst))
+        g.remote_dma_fused(trs, local_sem=T.sem.loc)
+        cnt["loc"] = cnt.get("loc", 0) + N - 1
+        cnt["arr%d" % t] = N - 1
+
+    def receive(t):
+        arr = ("arr%d" % t, N - 1)
+        if VIA_DRAM:
+            lastw["land%d" % t] = arr
+            for j, q in enumerate(dests):
+                dma("y" if j < 4 else "s", "inn%d" % t, T.win[15::16, 1024 + 128 * q:1024 + 128 * q + 128],
+                    T.land[8 * t + q], ["land%d" % t, "remfill"], ["remin%d" % j])
+        else:
+            lastw[remn(t) + "in"] = arr
+
+    def wreads(t):
+        if VIA_DRAM:
+            return WO + ["remin%d" % j for j in range(N - 1)] + ["rem0own", "remfill"]
+        return WO + [remn(t) + "in", remn(t) + "own"]
+
+    def own_piece(t):
+        gather("s", T.win[:, rem(t) + 128 * r:rem(t) + 128 * r + 128], own_win, T.osd[:, 56:64],
+               WO + OSD + ["remfill"], [remn(t) + "own"])
+
+    ST = ["stagea", "stageb"]
+    dma("y", "lsd", T.sdst[:], T.sd[:], [], ["sdst"])
+    dma("s", "lth", T.thst[:], T.th[:], [], ["thst"])
+    dma("s", "lth", T.nbst[:], T.nb[:], [], ["nbst"])
+    op("v", lambda: V.memset(T.stage[:, 0:768], 0), [], ["stagea"])
+    op("g", lambda: g.iota(T.stage[:, 768:1024], [[0, 256]], 0, 0), [], ["stageb"])
+    dma("y", "lst", T.stage[15::16, :], T.st[:], [], ST)
+    dma("y", "lpair", T.px[:, 0:4096], T.pair[:], [], ["px0"])
+    op("g", lambda: g.iota(T.dif[:], [[-1, 128]], 0, 1, allow_small_or_imprecise_dtypes=True), [], ["dif"])
+    op("g", lambda: g.iota(T.desc[:], [[0, 16], [-1, 16]], 15, 0, allow_small_or_imprecise_dtypes=True), [], ["desc"])
+    if VIA_DRAM:
+        op("v", lambda: V.memset(T.win[:, 1024:2048], 0.0), [], ["remfill"])
+    op("v", lambda: V.memset(T.sel[:], 0.0), [], ["sel0"])
+    op("v", lambda: V.memset(T.mn[:, 7::MW], 0.0), [], ["mn0", "mn1"])
+    op("v", lambda: V.tensor_scalar(T.idb[:], T.dif[:], 0.0, None, A.is_equal), ["dif"], ["idb"])
+    op("v", lambda: V.tensor_scalar(T.sel[:, 15:128:16], T.dif[:, 15:128:16], 0.0, None, A.is_equal), ["dif", "sel0"], ["selu"])
+    op("v", lambda: V.tensor_scalar(T.sel[:, 159:272:16], T.dif[:, 15:128:16], 0.0, 592.0, A.is_equal, A.mult),
+       ["dif", "sel0"], ["selz"])
+    k = 8 * (N - 1 - r)
+    if k:
+        copy("v", T.osd[:, 0:k], T.sdst[:, 64 - k:64], ["sdst"], ["osd0"])
+    copy("v", T.osd[:, k:64], T.sdst[:, 0:64 - k], ["sdst"], ["osd1"])
+    gather("v", T.snd[:, 0:896], T.stage[:, 0:1024], T.osd[:, 0:56], ST + OSD, ["snd0"])
+    send(0, lambda j: ["snd0"])
+
+    dma("y", "ltb", T.tbst[:], T.tb[:], [], ["tbst"])
+    dma("y", "lown", T.owns[:], T.own[:], [], ["owns"])
+    copy("v", own_win, T.stage[:], ST, WO)
+    own_piece(0)
+    copy("s", T.px[:, 8192:10240], T.px[:, 0:2048], ["px0"], ["px2"])
+    if not VIA_DRAM:
+        for nm in ("thst", "nbst"):
+            op("v", lambda: V.tensor_scalar(T[nm][:, 3:6], T[nm][:, 3:6], 1024, None, A.add), [nm], [nm])
+        for nm in ("thst", "nbst"):
+            op("v", lambda: V.tensor_scalar(T[nm][:, 3:6], T[nm][:, 3:6], 2047, None, A.bitwise_and), [nm], [nm])
+    for b in range(2):
+        copy("v", T.oth[:, 96 * b:96 * b + 96], T.thst[:, :, b, :], ["thst"], ["oth%d" % b])
+        copy("v", T.onb[:, 96 * b:96 * b + 96], T.nbst[:, :, b, :], ["nbst"], ["onb%d" % b])
+    op("v", lambda: V.tensor_scalar(T.rst[:], T.desc[:], 15.0, 2.0 ** 90, A.is_equal, A.mult), ["desc"], ["rst"])
+    op("v", lambda: V.tensor_scalar(T.idf[:], T.dif[:], 0.0, None, A.is_equal), ["dif"], ["idf"])
+    copy("v", T.px[:, 4096:8192], T.px[:, 0:4096], ["px0"], ["px1"])
+    copy("v", T.px[:, 12288:XW], T.px[:, 0:XW - 12288], ["px0"], ["px3"])
+    for b in range(2):
+        op("v", lambda: V.tensor_scalar(T.tb16[:, 96 * b:96 * b + 96], T.tbst[:, :, b, :], 16.0, None, A.mult),
+           ["tbst"], ["tb16%d" % b])
+    receive(0)
+    copy("s", T.px[:, 10240:12288], T.px[:, 2048:4096], ["px0"], ["px4"])
+    PX = ["px0", "px1", "px2", "px3", "px4"]
+
+    def pair_of(out, base, win, off, c0, cut, rd, name):
+        gather("v", out[:, base:base + 16 * cut], win, off[:, c0:c0 + cut], rd, [name + "v"])
+        gather("s", out[:, base + 16 * cut:base + 768], win, off[:, c0 + cut:c0 + 48], rd, [name + "s"])
+
+    pc, pe = [T.pc0, T.pc1], [T.pe0, T.pe1]
+    for t in range(RD):
+        h, last = t & 1, t == RD - 1
+        if t:
+            receive(t)
+        for b in range(2):
+            mms([(pc[b][:, 0:48], T.idb[:], T.tb16[:, 96 * b + 48 * h:96 * b + 48 * h + 48], True, False)],
+                ["idb", "tb16%d" % b], ["pc%d" % b])
+
+        def states(b, src, off, offn, so, seln, name, cut, stop):
+            pair_of(src, 768 * b, window(t), off, 96 * b + 48 * h, cut, wreads(t) + [offn + str(b)], name + str(b))
+            mms([(pc[b][:, 0:48], T.sel[:, so + 15 - i:so + 143 - i], src[:, 768 * b + i:768 * b + 768:16], False,
+                  stop and i == 15) for i in range(16)], [name + "%dv" % b, name + "%ds" % b, seln], ["pc%d" % b])
+
+        def to_offsets(b):
+            copy("v", T.col[:, 48 * b:48 * b + 48], pc[b][:, 0:48], [], ["pc%d" % b, "col%d" % b])
+
+        def energies(b):
+            items = []
+            for c in range(2):
+                o = pe[b][:, 128 * c:128 * c + 128]
+                a = 512 * h + 256 * b + 128 * c
+                items.append((o, T.owns[:, a:a + 128], T.idb[:], True, False))
+                for e in range(3):
+                    a = 768 * b + 256 * e + 128 * c
+                    items.append((o, T.xx[:, a:a + 128], T.idb[:], False, e == 2))
+            mms(items, ["owns", "idb", "x%dv" % b, "x%ds" % b], ["pe%d" % b])
+
+        def low(b):
+            op("v", lambda: V.tensor_tensor_scan(T.mn[:, MW * b + 8:MW * b + 264], T.rst[:], pe[b][:, 0:256], 0.0, A.add, A.min),
+               ["rst"], ["pe%d" % b, "mn%d" % b])
+
+        def first(b):
+            op("v", lambda: V.tensor_tensor(T.nlt[:, 256 * b:256 * b + 256], pe[b][:, 0:256],
+                                            T.mn[:, MW * b + 7:MW * b + 263], A.is_ge),
+               ["mn%d" % b], ["pe%d" % b, "nlt%d" % b])
+
+        def keep(b):
+            op("v", lambda: V.tensor_tensor_scan(T.arg[:, 256 * b:256 * b + 256], T.nlt[:, 256 * b:256 * b + 256],
+                                                 T.desc[:], 0.0, A.mult, A.max),
+               ["nlt%d" % b, "desc"], ["arg%d" % b])
+
+        def back(b, outs, names):
+            mms([(outs[c], T.arg[:, 256 * b + 128 * c:256 * b + 128 * c + 128], T.idb[:], True, True) for c in range(2)],
+                ["arg%d" % b, "idb"], names)
+
+        def turn_e(b, bank, name):
+            def fn():
+                P.transpose(bank[:, 0:128], T.mn[:, MW * b + 8:MW * b + 136], T.idf[:])
+                return P.transpose(bank[:, 128:256], T.mn[:, MW * b + 136:MW * b + 264], T.idf[:])
+            op("p", fn, ["mn%d" % b, "idf"], [name])
+
+        states(0, T.zz, T.oth, "oth", 144, "selz", "z", 24, False)
+        states(0, T.uu, T.onb, "onb", 0, "selu", "u", 24, True)
+        states(1, T.zz, T.oth, "oth", 144, "selz", "z", 24, False)
+        to_offsets(0)
+        states(1, T.uu, T.onb, "onb", 0, "selu", "u", 22, True)
+        pair_of(T.xx, 0, T.px[:, 0:XW], T.col, 0, 22, PX + ["col0"], "x0")
+        to_offsets(1)
+        energies(0)
+        pair_of(T.xx, 768, T.px[:, 0:XW], T.col, 48, 24, PX + ["col1"], "x1")
+        energies(1)
+        low(0)
+        if last:
+            turn_e(0, T.pt, "pt")
+        first(0)
+        low(1)
+        keep(0)
+        back(0, [T.pb0[:, 0:128], T.pb0[:, 128:256]], ["pb0"])
+        w0 = OWN + 512 * h
+        if not last:
+            flip("s", T.win[:, w0:w0 + 256], T.pb0[:, 0:256], [], ["pb0", "wa"])
+            first(1)
+            keep(1)
+            back(1, [T.pb1[:, 0:128], T.pb2[:, 0:128]], ["pb1", "pb2"])
+            flip("s", T.win[:, w0 + 256:w0 + 384], T.pb1[:, 0:128], [], ["pb1", "wb"])
+            flip("v", T.win[:, w0 + 384:w0 + 512], T.pb2[:, 0:128], [], ["pb2", "wc"])
+            s0 = 896 * (t + 1)
+            gather("v", T.snd[:, s0:s0 + 448], own_win, T.osd[:, 0:28], WO + OSD, ["sv%d" % t])
+            gather("s", T.snd[:, s0 + 448:s0 + 896], own_win, T.osd[:, 28:56], WO + OSD, ["ss%d" % t])
+            send(t + 1, lambda j: ["sv%d" % t] * (j <= 3) + ["ss%d" % t] * (j >= 3))
+            own_piece(t + 1)
+            if t == RD - 2:
+                turn_e(0, T.pt, "pt")
+                turn_e(1, T.pc0, "pc0")
+                copy("v", T.yo[:, 0:512], T.win[:, w0:w0 + 512], WO, ["yo2"])
+                dma("y", "oy2", T.y[:, 0:512], T.yo[15::16, 0:512], ["yo2"], [])
+                copy("v", T.eo[:, 0:256], T.pt[:, 0:256], [], ["pt", "eo2a"])
+                copy("v", T.eo[:, 256:512], T.pc0[:, 0:256], [], ["pc0", "eo2b"])
+                dma("y", "oe2", T.e[:, 0:512], T.eo[15::16, 0:512], ["eo2a", "eo2b"], [])
+        else:
+            turn_e(1, T.pc0, "pc0")
+            copy("s", T.eo[:, 512:768], T.pt[:, 0:256], [], ["pt", "eo3a"])
+            flip("s", T.yo[:, 512:768], T.pb0[:, 0:256], [], ["pb0", "yo3a"])
+            first(1)
+            keep(1)
+            back(1, [T.pb1[:, 0:128], T.pb1[:, 128:256]], ["pb1"])
+            copy("s", T.eo[:, 768:1024], T.pc0[:, 0:256], [], ["pc0", "eo3b"])
+            dma("s", "oe3", T.e[:, 512:1024], T.eo[15::16, 512:1024], ["eo3a", "eo3b"], [])
+            flip("v", T.yo[:, 768:1024], T.pb1[:, 0:256], [], ["pb1", "yo3b"])
+            dma("y", "oy3", T.y[:, 512:1024], T.yo[15::16, 512:1024], ["yo3a", "yo3b"], [])
+
+    late = ("oy3", "oe3")
+    for sem in [s for s in cnt if s not in late] + list(late):
+        if known["g"].get(sem, 0) < cnt[sem]:
+            g.wait_ge(T.sem[sem], cnt[sem])

@@ -2,46 +2,70 @@ from concourse.bass import DstId, RemoteDMATransfer
 from concourse.mybir import AluOpType, ActivationFunctionType
 
 N, RD = 8, 4
-VIA_DRAM = True
-XW = 16 * 255 + 592 * 15 + 16
-MW = 264
+NP = 256 + 15
+CFG = dict(ny=4, oq="y", ownearly=0, cc=50, n1=176, n0=9, last="", pick="v0-16 s40-56 y0 y1 y5 v16-28 s28-40 y2 y3 s4 s6", ps="vsvvv", pop="Z", bygroup=0, wq="yyyyyyy", fq="vyyygggg", order="""
+    Zv0-24 Zs24-48 P0-48 Yv0-24 Ys24-50 W0-48 Zv48-74 Zs74-96 P48-96 C0-48 Yv50-66 Ys66-96 W48-96
+    Xv0-24 Xs24-48 C48-96 E0 E1 Xv48-58 Xs58-72 E2 Xs72-96 L0-2 E3 F0-2 L2-3 K0-2 B0 B1 F2-3 Ts0-2
+    L3-4 K2-3 B2 F3-4 Ts2-3 K3-4 B3 Tv3-4""")
 
 SCRATCH = {
-    "stage": ("sbuf", [128, 1024], "int32"),
+    "stst": ("sbuf", [128, 64], "int32"),
+    "stb": ("sbuf", [128, 64], "bfloat16"),
+    "idp": ("sbuf", [128, 144], "bfloat16"),
     "sdst": ("sbuf", [128, 64], "int32"),
-    "thst": ("sbuf", [128, 6, 2, 16], "int32"),
-    "nbst": ("sbuf", [128, 6, 2, 16], "int32"),
-    "tbst": ("sbuf", [128, 6, 2, 16], "int32"),
+    "thst": ("sbuf", [128, 6, 4, 8], "int32"),
+    "nbst": ("sbuf", [128, 6, 4, 8], "int32"),
+    "tbst": ("sbuf", [128, 192], "int32"),
+    "tbm": ("sbuf", [128, 192], "int32"),
+    "tba": ("sbuf", [128, 6, 4, 8], "int32"),
     "osd": ("sbuf", [128, 64], "uint16"),
-    "oth": ("sbuf", [128, 192], "uint16"),
-    "onb": ("sbuf", [128, 192], "uint16"),
-    "tb16": ("sbuf", [128, 192], "bfloat16"),
+    "oth": ("sbuf", [128, 2, 96], "uint16"),
+    "onb": ("sbuf", [128, 2, 96], "uint16"),
+    "tb16": ("sbuf", [128, 2, 96], "bfloat16"),
     "col": ("sbuf", [128, 96], "uint16"),
-    "win": ("sbuf", [128, 3072], "bfloat16"),
-    "snd": ("sbuf", [128, 896 * RD], "bfloat16"),
+    "win": ("sbuf", [128, 2048], "bfloat16"),
+    "snd": ("sbuf", [128, 896 * 2], "bfloat16"),
+    "big": ("sbuf", [128, 1024 * N], "bfloat16"),
+    "tw": ("sbuf", [128, 2048], "bfloat16"),
+    "low": ("sbuf", [128, 256], "bfloat16"),
+    "mk": ("sbuf", [128, 8], "float32"),
+    "mi": ("sbuf", [128, 2], "int32"),
+    "sel2": ("sbuf", [128, 144], "bfloat16"),
+    "bth": ("sbuf", [128, 2, 96], "uint16"),
+    "bnb": ("sbuf", [128, 2, 96], "uint16"),
+    "outw": ("dram", [7, 128, 16], "bfloat16"),
+    "landw": ("dram", [8, 128, 16], "bfloat16"),
+    "land3": ("dram", [256, 128, 4], "bfloat16"),
+    "new": ("sbuf", [128, 512 * 3], "bfloat16"),
+    "land2": ("dram", [32, 128, 32], "bfloat16"),
+    "shst": ("sbuf", [128, 32], "int32"),
+    "shb": ("sbuf", [128, 32], "bfloat16"),
     "owns": ("sbuf", [128, 1024], "bfloat16"),
-    "px": ("sbuf", [128, XW], "bfloat16"),
+    "raw": ("sbuf", [128, 256, 16], "bfloat16"),
+    "px": ("sbuf", [128, NP * 16], "bfloat16"),
     "zz": ("sbuf", [128, 1536], "bfloat16"),
-    "uu": ("sbuf", [128, 1536], "bfloat16"),
+    "ww": ("sbuf", [128, 1536], "bfloat16"),
     "xx": ("sbuf", [128, 1536], "bfloat16"),
-    "dif": ("sbuf", [128, 128], "float32"),
+    "dif": ("sbuf", [128, 144], "float32"),
     "idb": ("sbuf", [128, 128], "bfloat16"),
     "idf": ("sbuf", [128, 128], "float32"),
-    "sel": ("sbuf", [128, 288], "bfloat16"),
+    "sel": ("sbuf", [128, 144], "bfloat16"),
     "desc": ("sbuf", [128, 256], "bfloat16"),
     "rst": ("sbuf", [128, 256], "bfloat16"),
-    "mn": ("sbuf", [128, 2 * MW], "float32"),
+    "mn": ("sbuf", [128, 520], "float32"),
     "nlt": ("sbuf", [128, 512], "bfloat16"),
     "arg": ("sbuf", [128, 512], "bfloat16"),
     "yo": ("sbuf", [128, 1024], "float32"),
-    "eo": ("sbuf", [128, 1024], "float32"),
-    "outd": ("dram", [7 * RD, 128, 8], "bfloat16"),
-    "land": ("dram", [8 * RD, 128, 8], "bfloat16"),
+    "eo": ("sbuf", [128, 384], "float32"),
+    "outd": ("dram", [7, 128, 8], "bfloat16"),
+    "land": ("dram", [8, 128, 8], "bfloat16"),
 }
-for _k in ("pc0", "pc1", "pe0", "pe1", "pb0", "pb1", "pb2", "pt"):
+for _k in ("pe0", "pe1"):
+    SCRATCH[_k] = ("psum", [128, 1024], "float32")
+for _k in ("pc0", "pc1", "pb0", "pb1"):
     SCRATCH[_k] = ("psum", [128, 512], "float32")
 
-SEMAPHORES = (["cv", "cs", "cp", "cg", "lsd", "lst", "lth", "ltb", "lown", "lpair", "loc", "oy2", "oe2", "oy3", "oe3"]
+SEMAPHORES = (["cv", "cs", "cp", "cg", "lsd", "lst", "lth", "ltb", "lown", "lpair", "loc", "early", "late", "outw", "arrw", "innw", "outi", "arri", "inni", "lsh", "lfill", "lbig"]
               + ["out%d" % t for t in range(RD)] + ["arr%d" % t for t in range(RD)] + ["inn%d" % t for t in range(RD)])
 
 
@@ -104,11 +128,13 @@ def rank_program(g, core, T, topo):
             c[k] = max(c.get(k, 0), n)
         note((sem, None), rd, wr)
 
-    def gather(q, out, win, off, rd, wr):
-        if q == "v":
-            op(q, lambda: V.tensor_copy(out, win.indirect(off)), rd, wr)
+    def gather(q, out, win, off, rd, wr, scale=None):
+        if q == "s":
+            op(q, lambda: S.activation(out, win.indirect(off), F.Copy, scale=scale or 1.0), rd, wr)
+        elif scale:
+            op(q, lambda: V.tensor_scalar(out, win.indirect(off), scale, None, A.mult), rd, wr)
         else:
-            op(q, lambda: S.activation(out, win.indirect(off), F.Copy), rd, wr)
+            op(q, lambda: V.tensor_copy(out, win.indirect(off)), rd, wr)
 
     def flip(q, out, in_, rd, wr):
         if q == "v":
@@ -130,221 +156,304 @@ def rank_program(g, core, T, topo):
             return last
         op("p", fn, rd, wr)
 
-    OWN = 0 if VIA_DRAM else 1024
-    WO = ["wa", "wb", "wc"]
+    def units(name, a, b):
+        return ["%s%d" % (name, k) for k in range(a // 2, b // 2)]
+
+    WO = ["w0", "w1", "w2", "w3"]
+    WALL = WO + ["remin%d" % j for j in range(N - 1)] + ["mine", "remfill"]
     OSD = ["osd0", "osd1"]
-
-    def rem(t):
-        return 1024 if VIA_DRAM else (2048 if t % 2 == 0 else 0)
-
-    def remn(t):
-        return "rem%d" % (0 if VIA_DRAM else t % 2)
-
-    def window(t):
-        a = 0 if (VIA_DRAM or t % 2) else 1024
-        return T.win[:, a:a + 2048]
-
+    BO = ["b0", "b1", "b2", "b3"]
+    FILL = ["fill%d" % j for j in range(N)]
+    BALL = FILL + ["bin%d" % j for j in range(N)] + ["sec%d" % j for j in range(N)]
+    later = []
+    TO = ["tw0", "tw1", "tw2", "tw3"]
+    TW = TO + ["twfill", "twmine"] + ["twin%d" % j for j in range(N - 1)]
     dests = [(r + 1 + j) % N for j in range(N - 1)]
-    own_win = T.win[:, OWN:OWN + 1024]
+    own_win = T.win[:, 0:1024]
 
-    def send(t, parts):
-        if VIA_DRAM:
-            for j in range(N - 1):
-                dma("y" if j < 4 else "s", "out%d" % t, T.outd[7 * t + j],
-                    T.snd[15::16, 896 * t + 128 * j:896 * t + 128 * j + 128], parts(j), ["od%d_%d" % (t, j)])
-            need("g", [("out%d" % t, None)])
-        else:
-            need("g", [lastw[x] for j in range(N - 1) for x in parts(j)])
+    def send(t):
+        for w in CFG["pick"].split():
+            q, a, b = w[0], int(w[1:].split("-")[0]), int(w[1:].split("-")[-1])
+            if "-" in w:
+                gather(q, T.snd[:, 896 * t + 16 * a:896 * t + 16 * b], own_win, T.osd[:, a:b], WO + OSD, units("s%d_" % t, a, b))
+            else:
+                dma(q, "out%d" % t, T.outd[7 * t + a], T.snd[15::16, 896 * t + 128 * a:896 * t + 128 * a + 128],
+                    units("s%d_" % t, 8 * a, 8 * a + 8), ["od%d_%d" % (t, a)])
+        remote("0", lambda j: T.outd[j], T.land[r])
+        gather("s", T.win[:, 1024 + 128 * r:1152 + 128 * r], own_win, T.osd[:, 56:64], WO + OSD + ["remfill"], ["mine"])
+
+    def remote(n, src, dst):
+        need("g", [("out" + n, None)])
         trs = []
         for j, d in enumerate(dests):
             c = T.cores[d]
             rid, pid = topo.addr(c, core)
-            if VIA_DRAM:
-                src, dst = T.outd[7 * t + j], T.land[8 * t + r]
-            else:
-                src = T.snd[:, 896 * t + 128 * j:896 * t + 128 * j + 128]
-                dst = T.win[:, rem(t) + 128 * r:rem(t) + 128 * r + 128]
             trs.append(RemoteDMATransfer(dst_ids=[DstId(rid=rid, pnc=pid)], dma_engine_mask=1 << topo.engines(core, c)[j],
-                                         remote_sem=T.sem["arr%d" % t], src=src, dst=dst))
+                                         remote_sem=T.sem["arr" + n], src=src(j), dst=dst))
         g.remote_dma_fused(trs, local_sem=T.sem.loc)
         cnt["loc"] = cnt.get("loc", 0) + N - 1
-        cnt["arr%d" % t] = N - 1
+        cnt["arr" + n] = N - 1
+
+    def span(t):
+        return 4096 * (1 - t % 2)
+
+    def share(n, k, src, rd):
+        if CFG["bygroup"]:
+            dma(CFG["oq"], "out" + n, T.land3[64 * k + r:64 * k + 64:8], src, rd, ["od" + n])
+            need("g", [("out" + n, None)])
+            ids = [DstId(rid=a, pnc=b) for a, b in [topo.addr(T.cores[d], core) for d in dests]]
+            engines = topo.engines(core, T.cores[dests[0]])
+            g.remote_dma_fused([RemoteDMATransfer(dst_ids=ids, dma_engine_mask=1 << engines[c], remote_sem=T.sem["arr" + n],
+                                                  srcs=[T.land3[64 * k + 8 * c + r]], dsts=[T.land3[64 * k + 8 * c + r]] * (N - 1))
+                                for c in range(8)], local_sem=T.sem.loc)
+            cnt["loc"] = cnt.get("loc", 0) + 8
+            cnt["arr" + n] = 8 * (N - 1)
+        else:
+            dma(CFG["oq"], "out" + n, T.land2[8 * k + r], src, rd, ["od" + n])
+            remote(n, lambda j: T.land2[8 * k + r], T.land2[8 * k + r])
+
+    def take(n, k, a, wr):
+        lastw["land" + n] = ("arr" + n, cnt["arr" + n])
+        if CFG["bygroup"]:
+            dma("y", "inn" + n, T.big[15::16, a:a + 4096], T.land3[64 * k:64 * k + 64], ["land" + n, "od" + n] + FILL, [wr + "0"])
+        else:
+            for j, q in enumerate([r] + dests):
+                dma("y" if j <= CFG["ny"] or n == "i" else "s", "inn" + n, T.big[15::16, a + 512 * q:a + 512 * q + 512], T.land2[8 * k + q],
+                    ["land" + n if j else "od" + n, FILL[(a + 512 * q) // 1024]], [wr + str(j)])
 
     def receive(t):
-        arr = ("arr%d" % t, N - 1)
-        if VIA_DRAM:
-            lastw["land%d" % t] = arr
-            for j, q in enumerate(dests):
-                dma("y" if j < 4 else "s", "inn%d" % t, T.win[15::16, 1024 + 128 * q:1024 + 128 * q + 128],
-                    T.land[8 * t + q], ["land%d" % t, "remfill"], ["remin%d" % j])
+        if t:
+            return take(str(t), t - 1, span(t), "bin")
+        lastw["land0"] = ("arr0", N - 1)
+        for j, q in enumerate(dests):
+            dma("y" if j < CFG["ny"] else "s", "inn0", T.win[15::16, 1024 + 128 * q:1024 + 128 * q + 128], T.land[q], ["land0", "remfill"], ["remin%d" % j])
+
+    def fill(j, q):
+        out = T.big[:, 1024 * j:1024 * j + 1024]
+        if q == "g":
+            op("g", lambda: g.iota(out, [[0, 1024]], 0, 0, allow_small_or_imprecise_dtypes=True), [], ["fill%d" % j])
+        elif q == "v":
+            op("v", lambda: V.memset(out, 0.0), [], ["fill%d" % j])
         else:
-            lastw[remn(t) + "in"] = arr
+            dma("y", "lfill", out, T.owns[:], ["owns"], ["fill%d" % j])
 
-    def wreads(t):
-        if VIA_DRAM:
-            return WO + ["remin%d" % j for j in range(N - 1)] + ["rem0own", "remfill"]
-        return WO + [remn(t) + "in", remn(t) + "own"]
+    def compose(h):
+        for src, off, name, out, bank in ((T.zz, T.oth, "z", T.bth, "pc0"), (T.ww, T.onb, "u", T.bnb, "pb1")):
+            for q, a, b in (("v", 0, CFG["cc"]), ("s", CFG["cc"], 96)):
+                gather(q, src[:, 16 * a:16 * b], T.tw[:, 0:2048], off[:, h, a:b], TW + LI["oth"] + LI["onb"], units(name, a, b))
+            mms([(T[bank][:, 0:96], T.sel2[:, 15 - i:143 - i], src[:, i:1536:16], i == 0, i == 15) for i in range(16)],
+                units(name, 0, 96) + ["sel2"], [bank])
+            if name == "z":
+                later.append(lambda: copy("v", T.bth[:, h, :], T.pc0[:, 0:96], [], ["pc0", "bth%d" % h]))
+            else:
+                later.pop()()
+                later.append(lambda: copy("v", T.bnb[:, h, :], T.pb1[:, 0:96], [], ["pb1", "bnb%d" % h]))
 
-    def own_piece(t):
-        gather("s", T.win[:, rem(t) + 128 * r:rem(t) + 128 * r + 128], own_win, T.osd[:, 56:64],
-               WO + OSD + ["remfill"], [remn(t) + "own"])
-
-    ST = ["stagea", "stageb"]
-    dma("y", "lsd", T.sdst[:], T.sd[:], [], ["sdst"])
-    dma("s", "lth", T.thst[:], T.th[:], [], ["thst"])
-    dma("s", "lth", T.nbst[:], T.nb[:], [], ["nbst"])
-    op("v", lambda: V.memset(T.stage[:, 0:768], 0), [], ["stagea"])
-    op("g", lambda: g.iota(T.stage[:, 768:1024], [[0, 256]], 0, 0), [], ["stageb"])
-    dma("y", "lst", T.stage[15::16, :], T.st[:], [], ST)
-    dma("y", "lpair", T.px[:, 0:4096], T.pair[:], [], ["px0"])
-    op("g", lambda: g.iota(T.dif[:], [[-1, 128]], 0, 1, allow_small_or_imprecise_dtypes=True), [], ["dif"])
+    dma("y", "lst", T.stst[:], T.st[:], [], ["stst"])
+    dma("s", "lsd", T.sdst[:], T.sd[:], [], ["sdst"])
+    dma("s", "lsh", T.shst[:], T.st[:, 512:1024], [], ["shst"])
+    n1 = CFG["n1"]
+    dma("y", "lpair", T.raw[:, 0:n1, :], T.pair[:, 0:16 * n1], [], ["raw0"])
+    op("g", lambda: g.iota(T.dif[:], [[-1, 144]], 15, 1, allow_small_or_imprecise_dtypes=True), [], ["dif"])
+    op("g", lambda: g.iota(T.mi[:, 0:1], [[0, 1]], 0, 1), [], ["mi0"])
+    op("g", lambda: g.iota(T.low[:], [[1, 256]], 0, 0, allow_small_or_imprecise_dtypes=True), [], ["low"])
     op("g", lambda: g.iota(T.desc[:], [[0, 16], [-1, 16]], 15, 0, allow_small_or_imprecise_dtypes=True), [], ["desc"])
-    if VIA_DRAM:
-        op("v", lambda: V.memset(T.win[:, 1024:2048], 0.0), [], ["remfill"])
-    op("v", lambda: V.memset(T.sel[:], 0.0), [], ["sel0"])
-    op("v", lambda: V.memset(T.mn[:, 7::MW], 0.0), [], ["mn0", "mn1"])
-    op("v", lambda: V.tensor_scalar(T.idb[:], T.dif[:], 0.0, None, A.is_equal), ["dif"], ["idb"])
-    op("v", lambda: V.tensor_scalar(T.sel[:, 15:128:16], T.dif[:, 15:128:16], 0.0, None, A.is_equal), ["dif", "sel0"], ["selu"])
-    op("v", lambda: V.tensor_scalar(T.sel[:, 159:272:16], T.dif[:, 15:128:16], 0.0, 592.0, A.is_equal, A.mult),
-       ["dif", "sel0"], ["selz"])
+    op("v", lambda: V.memset(T.win[:, 1024:2048], 0.0), [], ["remfill"])
+    copy("s", T.tw[:, 1024:2048], T.win[:, 1024:2048], ["remfill"], ["twfill"])
+    op("v", lambda: V.tensor_scalar(T.idp[:], T.dif[:], 0.0, None, A.is_equal), ["dif"], ["idp"])
+    op("v", lambda: V.tensor_scalar(T.mi[:, 1:2], T.mi[:, 0:1], 8, None, A.bitwise_and), ["mi0"], ["mi1"])
+    op("v", lambda: V.memset(T.sel[:], 0.0), [], ["sel"])
+    op("v", lambda: V.tensor_scalar(T.mk[:, 0:1], T.mi[:, 1:2], 0.125, None, A.mult), ["mi1"], ["mk0"])
+    op("v", lambda: V.tensor_scalar(T.mk[:, 1:2], T.mi[:, 1:2], -0.125, 1.0, A.mult, A.add), ["mi1"], ["mk1"])
+    op("v", lambda: V.memset(T.sel2[:], 0.0), [], ["sel2"])
+    op("v", lambda: V.memset(T.mn[:, 7:8], 0.0), [], ["mn0"])
+    op("v", lambda: V.tensor_scalar(T.sel[:, 15:128:16], T.dif[:, 30:143:16], 0.0, None, A.is_equal), ["dif"], ["sel"])
+    for j in range(2):
+        op("v", lambda: V.tensor_scalar(T.mk[:, 2 + 2 * j:4 + 2 * j], T.low[:, 0:2], 2.0 * r + 16 * j, T.mk[:, 1:2], A.add, A.mult),
+           ["low", "mk1"], ["mk2%d" % j])
+
+    def numbers(j):
+        op("v", lambda: V.tensor_scalar(T.tw[:, 256 * j:256 * j + 256], T.low[:], T.mk[:, 0:1], T.mk[:, 2 + j:3 + j], A.mult, A.add),
+           ["low", "mk0", "mk20", "mk21"], ["tw%d" % j])
+    copy("v", T.stb[:], T.stst[:], ["stst"], ["stb"])
+    copy("v", T.shb[:], T.shst[:], ["shst"], ["shb"])
+    share("i", 3, T.shb[:], ["shb"])
+    dma("y", "lpair", T.raw[:, n1:256, :], T.pair[:, 16 * n1:4096], [], ["raw1"])
     k = 8 * (N - 1 - r)
     if k:
         copy("v", T.osd[:, 0:k], T.sdst[:, 64 - k:64], ["sdst"], ["osd0"])
     copy("v", T.osd[:, k:64], T.sdst[:, 0:64 - k], ["sdst"], ["osd1"])
-    gather("v", T.snd[:, 0:896], T.stage[:, 0:1024], T.osd[:, 0:56], ST + OSD, ["snd0"])
-    send(0, lambda j: ["snd0"])
+    numbers(0)
+    numbers(1)
+    for b, (q, n) in enumerate((("s", CFG["n0"]), ("v", 16 - CFG["n0"]))):
+        j0, bank = b * CFG["n0"], T["pe%d" % b]
+        mms([(bank[:, 64 * j:64 * j + 64], T.idp[:, j0 + j:j0 + j + 128], T.stb[:], True, True) for j in range(n)],
+            ["stb", "idp"], ["pe%d" % (2 * b), "pe%d" % (2 * b + 1)])
+        copy(q, T.win[:, 64 * j0:64 * (j0 + n)], bank[:, 0:64 * n], [], ["pe%d" % (2 * b), "pe%d" % (2 * b + 1)] + WO[2 * b:2 * b + 2])
+    send(0)
 
     dma("y", "ltb", T.tbst[:], T.tb[:], [], ["tbst"])
-    dma("y", "lown", T.owns[:], T.own[:], [], ["owns"])
-    copy("v", own_win, T.stage[:], ST, WO)
-    own_piece(0)
-    copy("s", T.px[:, 8192:10240], T.px[:, 0:2048], ["px0"], ["px2"])
-    if not VIA_DRAM:
-        for nm in ("thst", "nbst"):
-            op("v", lambda: V.tensor_scalar(T[nm][:, 3:6], T[nm][:, 3:6], 1024, None, A.add), [nm], [nm])
-        for nm in ("thst", "nbst"):
-            op("v", lambda: V.tensor_scalar(T[nm][:, 3:6], T[nm][:, 3:6], 2047, None, A.bitwise_and), [nm], [nm])
-    for b in range(2):
-        copy("v", T.oth[:, 96 * b:96 * b + 96], T.thst[:, :, b, :], ["thst"], ["oth%d" % b])
-        copy("v", T.onb[:, 96 * b:96 * b + 96], T.nbst[:, :, b, :], ["nbst"], ["onb%d" % b])
+    dma("y", "lth", T.thst[:], T.th[:], [], ["thst"])
+    dma("y", "lth", T.nbst[:], T.nb[:], [], ["nbst"])
+    if CFG["ownearly"]:
+        dma("y", "lown", T.owns[:], T.own[:], [], ["owns"])
+    numbers(2)
+    numbers(3)
+    gather("s", T.snd[:, 896:1792], T.tw[:, 0:1024], T.osd[:, 0:56], TO + OSD, ["sws"])
+    for j in range(N - 1):
+        dma(CFG["wq"][j], "outw", T.outw[j], T.snd[7::8, 896 + 128 * j:1024 + 128 * j], ["sws"], ["ow%d" % j])
+    if "g" not in CFG["ps"]:
+        fill(7, "g")
+        remote("w", lambda j: T.outw[j], T.landw[r])
+    op("v", lambda: V.tensor_scalar(T.idb[:], T.dif[:, 15:143], 0.0, None, A.is_equal), ["dif"], ["idb"])
+    op("v", lambda: V.tensor_scalar(T.idf[:], T.dif[:, 15:143], 0.0, None, A.is_equal), ["dif"], ["idf"])
     op("v", lambda: V.tensor_scalar(T.rst[:], T.desc[:], 15.0, 2.0 ** 90, A.is_equal, A.mult), ["desc"], ["rst"])
-    op("v", lambda: V.tensor_scalar(T.idf[:], T.dif[:], 0.0, None, A.is_equal), ["dif"], ["idf"])
-    copy("v", T.px[:, 4096:8192], T.px[:, 0:4096], ["px0"], ["px1"])
-    copy("v", T.px[:, 12288:XW], T.px[:, 0:XW - 12288], ["px0"], ["px3"])
-    for b in range(2):
-        op("v", lambda: V.tensor_scalar(T.tb16[:, 96 * b:96 * b + 96], T.tbst[:, :, b, :], 16.0, None, A.mult),
-           ["tbst"], ["tb16%d" % b])
-    receive(0)
-    copy("s", T.px[:, 10240:12288], T.px[:, 2048:4096], ["px0"], ["px4"])
-    PX = ["px0", "px1", "px2", "px3", "px4"]
+    op("v", lambda: V.tensor_scalar(T.sel2[:, 15:128:16], T.dif[:, 30:143:16], -8.0, 256.0, A.is_equal, A.mult), ["dif"], ["sel2"])
+    op("v", lambda: V.tensor_tensor(T.sel2[:, 15:128:16], T.sel2[:, 15:128:16], T.sel[:, 15:128:16], A.add), ["sel"], ["sel2"])
+    PX = []
+    a = 0
+    while a < NP:
+        t0 = 37 * a % 256
+        n = min((255 - t0) // 37 + 1, NP - a)
+        q = CFG["ps"][len(PX) % len(CFG["ps"])]
+        PX.append("px%d" % a)
+        o, i = T.px[:, 16 * a:16 * (a + n)], T.raw[:, t0:t0 + 37 * (n - 1) + 1:37, :]
+        if q == "g":
+            op("g", lambda: g.affine_select(o, i, [[0, 16 * n]], A.is_ge, 0.0, 0, 0), ["raw0", "raw1"], PX[-1:])
+        else:
+            copy(q, o, i, ["raw0", "raw1"], PX[-1:])
+        a += n
+    if "g" in CFG["ps"]:
+        remote("w", lambda j: T.outw[j], T.landw[r])
+        fill(7, "g")
+    op("v", lambda: V.tensor_scalar(T.tbm[:], T.tbst[:], 173, None, A.mult), ["tbst"], ["tbm"])
+    for q in range(4):
+        copy("v", T.oth[:, :, 24 * q:24 * q + 24], T.thst[:, :, q, :], ["thst"], ["oth%d" % q])
+    op("v", lambda: V.tensor_scalar(T.tba[:], T.tbm[:], 255, None, A.bitwise_and), ["tbm"], ["tba"])
+    for q in range(4):
+        copy("v", T.onb[:, :, 24 * q:24 * q + 24], T.nbst[:, :, q, :], ["nbst"], ["onb%d" % q])
+    for q in range(4):
+        op("v", lambda: V.tensor_scalar(T.tb16[:, :, 24 * q:24 * q + 24], T.tba[:, :, q, :], 16.0, None, A.mult), ["tba"], ["tb16%d" % q])
+    LI = {n: [n + str(q) for q in range(4)] for n in ("oth", "onb", "tb16")}
 
-    def pair_of(out, base, win, off, c0, cut, rd, name):
-        gather("v", out[:, base:base + 16 * cut], win, off[:, c0:c0 + cut], rd, [name + "v"])
-        gather("s", out[:, base + 16 * cut:base + 768], win, off[:, c0 + cut:c0 + 48], rd, [name + "s"])
+    def places():
+        lastw["landw"] = ("arrw", N - 1)
+        for j, q in enumerate(dests):
+            dma("y", "innw", T.tw[7::8, 1024 + 128 * q:1152 + 128 * q], T.landw[q], ["landw", "twfill"], ["twin%d" % j])
+        for j in range(N - 2, -1, -1):
+            if CFG["fq"][j] != "v":
+                fill(j, CFG["fq"][j])
 
-    pc, pe = [T.pc0, T.pc1], [T.pe0, T.pe1]
+    def pe(a, b):
+        return T["pe%d" % (a // 2)][:, 384 + 128 * (a % 2):384 + 128 * (a % 2 + b - a)]
+
+    def chunks(name, a, b):
+        return [name + str(c) for c in range(a, b)]
+
     for t in range(RD):
         h, last = t & 1, t == RD - 1
+        w0 = 512 * h
+        blocks = {}
+
+        def energies_out(a, b, bank, q, dq, sem):
+            m, o = 8 * (b - a), 0 if sem == "early" else 128 + 64 * a
+            op("p", lambda: P.transpose(T[bank][0:m, 128:256], T.mn[:, 23 + 128 * a:8 + 128 * b:16], T.idf[:]),
+               ["mn%d" % c for c in range(a, b)] + ["idf"], [bank])
+            copy(q, T.eo[0:m, o:o + 128], T[bank][0:m, 128:256], [], [bank, "eo%d" % o])
+            for c in range(a, b):
+                dma(dq[c - a], sem, T.e[:, w0 + 128 * c:w0 + 128 * c + 128], T.eo[8 * (c - a):8 * (c - a) + 8, o:o + 128], ["eo%d" % o], [])
+
+        def step(w):
+            kind, q = w[0], w[1] if w[1] in "vs" else "v"
+            nums = [int(x) for x in w.lstrip("ZUWCXELFKYPBTvs").split("-")]
+            a, b = nums[0], nums[-1]
+            if later and kind == CFG["pop"]:
+                later.pop()()
+            if kind == "Z":
+                if t:
+                    gather(q, T.zz[:, 16 * a:16 * b], T.big[:, 0:1024 * N], T.bth[:, h, a:b], BALL + ["bth%d" % h], units("z", a, b), 16.0)
+                else:
+                    gather(q, T.zz[:, 16 * a:16 * b], T.win[:, 0:2048], T.oth[:, h, a:b], WALL + LI["oth"], units("z", a, b), 16.0)
+            elif kind == "W":
+                bank = blocks[a]
+                mms([(T[bank][:, 0:b - a], T.sel[:, 15 - i:143 - i], T.ww[:, 16 * a + i:16 * b:16], False, i == 15) for i in range(16)],
+                    units("u", a, b) + ["sel"], [bank])
+            elif kind == "C":
+                bank = blocks[a]
+                copy("v", T.col[:, a:b], T[bank][:, 0:b - a], [], [bank] + units("c", a, b))
+            elif kind == "X":
+                gather(q, T.xx[:, 16 * a:16 * b], T.px[:, 0:16 * NP], T.col[:, a:b], PX + units("c", a, b), units("x", a, b))
+            elif kind == "E":
+                mms([(pe(a, a + 1), T.xx[:, 384 * a + 128 * e:384 * a + 128 * e + 128], T.idb[:], False, e == 2) for e in range(3)],
+                    units("x", 24 * a, 24 * a + 24) + ["idb"], ["pe%d" % a])
+            elif kind == "L":
+                op("v", lambda: V.tensor_tensor_scan(T.mn[:, 8 + 128 * a:8 + 128 * b], T.rst[:, 0:128 * (b - a)], pe(a, b), 0.0, A.add, A.min),
+                   ["rst"], chunks("pe", a, b) + chunks("mn", a, b))
+                if last and b % 2 == 0:
+                    energies_out(b - 2, b, "pc%d" % (a // 2), "s", "ys", "late")
+            elif kind == "F":
+                op("v", lambda: V.tensor_tensor(T.nlt[:, 128 * a:128 * b], pe(a, b), T.mn[:, 7 + 128 * a:7 + 128 * b], A.is_ge),
+                   chunks("mn", max(a - 1, 0), b), chunks("pe", a, b) + chunks("nlt", a, b))
+            elif kind == "K":
+                op("v", lambda: V.tensor_tensor_scan(T.arg[:, 128 * a:128 * b], T.nlt[:, 128 * a:128 * b], T.desc[:, 0:128 * (b - a)], 0.0, A.mult, A.max),
+                   chunks("nlt", a, b) + ["desc"], chunks("arg", a, b))
+            elif kind == "Y":
+                if t:
+                    gather(q, T.ww[:, 16 * a:16 * b], T.big[:, 0:1024 * N], T.bnb[:, h, a:b], BALL + ["bnb%d" % h], units("u", a, b))
+                else:
+                    gather(q, T.ww[:, 16 * a:16 * b], T.win[:, 0:2048], T.onb[:, h, a:b], WALL + LI["onb"], units("u", a, b))
+            elif kind == "P":
+                bank = blocks[a]
+                mms([(T[bank][:, 0:b - a], T.sel[:, 15 - i:143 - i], T.zz[:, 16 * a + i:16 * b:16], False, False) for i in range(16)],
+                    units("z", a, b) + ["sel"], [bank])
+            elif kind == "B":
+                bank = ["pb0", "pb0", "pb1", "pb0"][a]
+                mms([(T[bank][:, 128 * a:128 * a + 128], T.arg[:, 128 * a:128 * a + 128], T.idb[:], True, True)], ["arg%d" % a, "idb"], [bank])
+            elif kind == "T":
+                bank = ["pb0", "pb0", "pb1", "pb0"][a]
+                c0, c1 = w0 + 128 * a, w0 + 128 * b
+                if last:
+                    flip(q, T.yo[:, c0:c1], T[bank][:, 128 * a:128 * b], [], [bank, "yo%d" % a])
+                    dma("s" if q == "s" else "y", "late", T.y[:, c0:c1], T.yo[15::16, c0:c1], ["yo%d" % a], [])
+                else:
+                    flip(q, T.new[:, 512 * t + 128 * a:512 * t + 128 * b], T[bank][:, 128 * a:128 * b], [], [bank] + BO[a:b])
+
+        order = (last and CFG["last"] or CFG["order"]).split()
+        for j, w in enumerate([w for w in order if w[0] == "W"]):
+            a, b = [int(x) for x in w[1:].split("-")]
+            blocks[a] = ["pc0", "pc1", "pb1"][j]
+            mms([(T[blocks[a]][:, 0:b - a], T.idb[:], T.tb16[:, h, a:b], True, False)], ["idb"] + LI["tb16"], [blocks[a]])
+
+        def alone():
+            for q in range(4):
+                mms([(pe(q, q + 1), T.owns[:, w0 + 128 * q:w0 + 128 * q + 128], T.idb[:], True, False)], ["owns", "idb"], ["pe%d" % q])
         if t:
-            receive(t)
-        for b in range(2):
-            mms([(pc[b][:, 0:48], T.idb[:], T.tb16[:, 96 * b + 48 * h:96 * b + 48 * h + 48], True, False)],
-                ["idb", "tb16%d" % b], ["pc%d" % b])
-
-        def states(b, src, off, offn, so, seln, name, cut, stop):
-            pair_of(src, 768 * b, window(t), off, 96 * b + 48 * h, cut, wreads(t) + [offn + str(b)], name + str(b))
-            mms([(pc[b][:, 0:48], T.sel[:, so + 15 - i:so + 143 - i], src[:, 768 * b + i:768 * b + 768:16], False,
-                  stop and i == 15) for i in range(16)], [name + "%dv" % b, name + "%ds" % b, seln], ["pc%d" % b])
-
-        def to_offsets(b):
-            copy("v", T.col[:, 48 * b:48 * b + 48], pc[b][:, 0:48], [], ["pc%d" % b, "col%d" % b])
-
-        def energies(b):
-            items = []
-            for c in range(2):
-                o = pe[b][:, 128 * c:128 * c + 128]
-                a = 512 * h + 256 * b + 128 * c
-                items.append((o, T.owns[:, a:a + 128], T.idb[:], True, False))
-                for e in range(3):
-                    a = 768 * b + 256 * e + 128 * c
-                    items.append((o, T.xx[:, a:a + 128], T.idb[:], False, e == 2))
-            mms(items, ["owns", "idb", "x%dv" % b, "x%ds" % b], ["pe%d" % b])
-
-        def low(b):
-            op("v", lambda: V.tensor_tensor_scan(T.mn[:, MW * b + 8:MW * b + 264], T.rst[:], pe[b][:, 0:256], 0.0, A.add, A.min),
-               ["rst"], ["pe%d" % b, "mn%d" % b])
-
-        def first(b):
-            op("v", lambda: V.tensor_tensor(T.nlt[:, 256 * b:256 * b + 256], pe[b][:, 0:256],
-                                            T.mn[:, MW * b + 7:MW * b + 263], A.is_ge),
-               ["mn%d" % b], ["pe%d" % b, "nlt%d" % b])
-
-        def keep(b):
-            op("v", lambda: V.tensor_tensor_scan(T.arg[:, 256 * b:256 * b + 256], T.nlt[:, 256 * b:256 * b + 256],
-                                                 T.desc[:], 0.0, A.mult, A.max),
-               ["nlt%d" % b, "desc"], ["arg%d" % b])
-
-        def back(b, outs, names):
-            mms([(outs[c], T.arg[:, 256 * b + 128 * c:256 * b + 128 * c + 128], T.idb[:], True, True) for c in range(2)],
-                ["arg%d" % b, "idb"], names)
-
-        def turn_e(b, bank, name):
-            def fn():
-                P.transpose(bank[:, 0:128], T.mn[:, MW * b + 8:MW * b + 136], T.idf[:])
-                return P.transpose(bank[:, 128:256], T.mn[:, MW * b + 136:MW * b + 264], T.idf[:])
-            op("p", fn, ["mn%d" % b, "idf"], [name])
-
-        states(0, T.zz, T.oth, "oth", 144, "selz", "z", 24, False)
-        states(0, T.uu, T.onb, "onb", 0, "selu", "u", 24, True)
-        states(1, T.zz, T.oth, "oth", 144, "selz", "z", 24, False)
-        to_offsets(0)
-        states(1, T.uu, T.onb, "onb", 0, "selu", "u", 22, True)
-        pair_of(T.xx, 0, T.px[:, 0:XW], T.col, 0, 22, PX + ["col0"], "x0")
-        to_offsets(1)
-        energies(0)
-        pair_of(T.xx, 768, T.px[:, 0:XW], T.col, 48, 24, PX + ["col1"], "x1")
-        energies(1)
-        low(0)
-        if last:
-            turn_e(0, T.pt, "pt")
-        first(0)
-        low(1)
-        keep(0)
-        back(0, [T.pb0[:, 0:128], T.pb0[:, 128:256]], ["pb0"])
-        w0 = OWN + 512 * h
+            alone()
+        receive(t)
+        if t == 0:
+            need("y", [("inn0", None)])
+            if not CFG["ownearly"]:
+                dma("y", "lown", T.owns[:], T.own[:], [], ["owns"])
+            places()
+        for w in order:
+            if t == 0 and w == "E0":
+                alone()
+            step(w)
         if not last:
-            flip("s", T.win[:, w0:w0 + 256], T.pb0[:, 0:256], [], ["pb0", "wa"])
-            first(1)
-            keep(1)
-            back(1, [T.pb1[:, 0:128], T.pb2[:, 0:128]], ["pb1", "pb2"])
-            flip("s", T.win[:, w0 + 256:w0 + 384], T.pb1[:, 0:128], [], ["pb1", "wb"])
-            flip("v", T.win[:, w0 + 384:w0 + 512], T.pb2[:, 0:128], [], ["pb2", "wc"])
-            s0 = 896 * (t + 1)
-            gather("v", T.snd[:, s0:s0 + 448], own_win, T.osd[:, 0:28], WO + OSD, ["sv%d" % t])
-            gather("s", T.snd[:, s0 + 448:s0 + 896], own_win, T.osd[:, 28:56], WO + OSD, ["ss%d" % t])
-            send(t + 1, lambda j: ["sv%d" % t] * (j <= 3) + ["ss%d" % t] * (j >= 3))
-            own_piece(t + 1)
+            share(str(t + 1), t, T.new[15::16, 512 * t:512 * t + 512], BO)
+            if t == 0:
+                for j in range(N):
+                    if CFG["fq"][j] == "v":
+                        fill(j, "v")
+                take("i", 3, 4096, "sec")
+                gather("s", T.tw[:, 1024 + 128 * r:1152 + 128 * r], T.tw[:, 0:1024], T.osd[:, 56:64], TO + OSD + ["twfill"], ["twmine"])
+            if t < 2:
+                compose(1 - t)
             if t == RD - 2:
-                turn_e(0, T.pt, "pt")
-                turn_e(1, T.pc0, "pc0")
-                copy("v", T.yo[:, 0:512], T.win[:, w0:w0 + 512], WO, ["yo2"])
-                dma("y", "oy2", T.y[:, 0:512], T.yo[15::16, 0:512], ["yo2"], [])
-                copy("v", T.eo[:, 0:256], T.pt[:, 0:256], [], ["pt", "eo2a"])
-                copy("v", T.eo[:, 256:512], T.pc0[:, 0:256], [], ["pc0", "eo2b"])
-                dma("y", "oe2", T.e[:, 0:512], T.eo[15::16, 0:512], ["eo2a", "eo2b"], [])
-        else:
-            turn_e(1, T.pc0, "pc0")
-            copy("s", T.eo[:, 512:768], T.pt[:, 0:256], [], ["pt", "eo3a"])
-            flip("s", T.yo[:, 512:768], T.pb0[:, 0:256], [], ["pb0", "yo3a"])
-            first(1)
-            keep(1)
-            back(1, [T.pb1[:, 0:128], T.pb1[:, 128:256]], ["pb1"])
-            copy("s", T.eo[:, 768:1024], T.pc0[:, 0:256], [], ["pc0", "eo3b"])
-            dma("s", "oe3", T.e[:, 512:1024], T.eo[15::16, 512:1024], ["eo3a", "eo3b"], [])
-            flip("v", T.yo[:, 768:1024], T.pb1[:, 0:256], [], ["pb1", "yo3b"])
-            dma("y", "oy3", T.y[:, 512:1024], T.yo[15::16, 512:1024], ["yo3a", "yo3b"], [])
+                copy("v", T.yo[:, 0:512], T.new[:, 512 * t:512 * t + 512], BO, ["yoe"])
+                dma("y", "early", T.y[:, 0:512], T.yo[15::16, 0:512], ["yoe"], [])
+                energies_out(0, 4, "pb1", "v", "yyyy", "early")
 
-    late = ("oy3", "oe3")
-    for sem in [s for s in cnt if s not in late] + list(late):
+    for sem in [s for s in cnt if s != "late"] + ["late"]:
         if known["g"].get(sem, 0) < cnt[sem]:
             g.wait_ge(T.sem[sem], cnt[sem])

@@ -3,28 +3,24 @@ from concourse.mybir import AluOpType, ActivationFunctionType
 
 N, RD = 8, 4
 NP = 256 + 15
-CFG = dict(ny=4, oq="y", ownearly=0, cc=50, n1=176, n0=9, last="", pick="v0-16 s40-56 y0 y1 y5 v16-28 s28-40 y2 y3 s4 s6", ps="vsvvv", pop="Z", bygroup=0, wq="yyyyyyy", fq="vyyygggg", order="""
-    Zv0-24 Zs24-48 P0-48 Yv0-24 Ys24-50 W0-48 Zv48-74 Zs74-96 P48-96 C0-48 Yv50-66 Ys66-96 W48-96
-    Xv0-24 Xs24-48 C48-96 E0 E1 Xv48-58 Xs58-72 E2 Xs72-96 L0-2 E3 F0-2 L2-3 K0-2 B0 B1 F2-3 Ts0-2
-    L3-4 K2-3 B2 F3-4 Ts2-3 K3-4 B3 Tv3-4""")
+CFG = dict(ny=4, oq="y", ownearly=0, cc=24, f1=1, sat="pc1", cut=[3840, 4480, 4480, 5504, 6912, 8192, 8192], m=[4, 2], hq=["yyyy", "yyyy"], wlate=1, n0=9, last="", pick="v0-16 s40-56 y0 y1 y5 v16-28 s28-40 y2 y3 s4 s6", ps="vsvvlvvv", pop="Y", yq="yysy", eq="yyyy", aat="E0", bygroup=1, wq="yyyyyyy", fq="eeyyyggg", order="""
+    Zv0-24 Zs24-48 P0-48 Yv0-24 Ys24-48 W0-48 Zv48-74 Zs74-96 P48-96 C0-48 Yv48-66 Ys66-96 W48-96
+    Xv0-24 Xs24-48 C48-96 E0 E1 Xv48-58 Xs58-72 E2 Xs72-96 L0-2 Os0-2 E3 F0-2 L2-3 K0-2 B0 B1 F2-3 Ts0-2
+    L3-4 Os2-4 K2-3 B2 F3-4 Ts2-3 K3-4 B3 Tv3-4""")
 
 SCRATCH = {
     "stst": ("sbuf", [128, 64], "int32"),
     "stb": ("sbuf", [128, 64], "bfloat16"),
     "idp": ("sbuf", [128, 144], "bfloat16"),
     "sdst": ("sbuf", [128, 64], "int32"),
-    "thst": ("sbuf", [128, 6, 4, 8], "int32"),
-    "nbst": ("sbuf", [128, 6, 4, 8], "int32"),
+    "lists": ("sbuf", [128, 12, 4, 8], "int32"),
+    "olist": ("sbuf", [128, 4, 96], "uint16"),
     "tbst": ("sbuf", [128, 192], "int32"),
     "tbm": ("sbuf", [128, 192], "int32"),
     "tba": ("sbuf", [128, 6, 4, 8], "int32"),
     "osd": ("sbuf", [128, 64], "uint16"),
-    "oth": ("sbuf", [128, 2, 96], "uint16"),
-    "onb": ("sbuf", [128, 2, 96], "uint16"),
     "tb16": ("sbuf", [128, 2, 96], "bfloat16"),
     "col": ("sbuf", [128, 96], "uint16"),
-    "win": ("sbuf", [128, 2048], "bfloat16"),
-    "snd": ("sbuf", [128, 896 * 2], "bfloat16"),
     "big": ("sbuf", [128, 1024 * N], "bfloat16"),
     "tw": ("sbuf", [128, 2048], "bfloat16"),
     "low": ("sbuf", [128, 256], "bfloat16"),
@@ -35,11 +31,13 @@ SCRATCH = {
     "bnb": ("sbuf", [128, 2, 96], "uint16"),
     "outw": ("dram", [7, 128, 16], "bfloat16"),
     "landw": ("dram", [8, 128, 16], "bfloat16"),
-    "land3": ("dram", [256, 128, 4], "bfloat16"),
+    "land3": ("dram", [128, 128, 2], "int32"),
+    "landi": ("dram", [16, 128, 8], "int32"),
+    "part0": ("dram", [192 // CFG["m"][0], 128, 2 * CFG["m"][0]], "bfloat16"),
+    "part1": ("dram", [192 // CFG["m"][1], 128, 2 * CFG["m"][1]], "bfloat16"),
     "new": ("sbuf", [128, 512 * 3], "bfloat16"),
-    "land2": ("dram", [32, 128, 32], "bfloat16"),
-    "shst": ("sbuf", [128, 32], "int32"),
-    "shb": ("sbuf", [128, 32], "bfloat16"),
+    "shst": ("sbuf", [128, 256], "int32"),
+    "shb": ("sbuf", [128, 256], "bfloat16"),
     "owns": ("sbuf", [128, 1024], "bfloat16"),
     "raw": ("sbuf", [128, 256, 16], "bfloat16"),
     "px": ("sbuf", [128, NP * 16], "bfloat16"),
@@ -47,7 +45,6 @@ SCRATCH = {
     "ww": ("sbuf", [128, 1536], "bfloat16"),
     "xx": ("sbuf", [128, 1536], "bfloat16"),
     "dif": ("sbuf", [128, 144], "float32"),
-    "idb": ("sbuf", [128, 128], "bfloat16"),
     "idf": ("sbuf", [128, 128], "float32"),
     "sel": ("sbuf", [128, 144], "bfloat16"),
     "desc": ("sbuf", [128, 256], "bfloat16"),
@@ -65,8 +62,8 @@ for _k in ("pe0", "pe1"):
 for _k in ("pc0", "pc1", "pb0", "pb1"):
     SCRATCH[_k] = ("psum", [128, 512], "float32")
 
-SEMAPHORES = (["cv", "cs", "cp", "cg", "lsd", "lst", "lth", "ltb", "lown", "lpair", "loc", "early", "late", "outw", "arrw", "innw", "outi", "arri", "inni", "lsh", "lfill", "lbig"]
-              + ["out%d" % t for t in range(RD)] + ["arr%d" % t for t in range(RD)] + ["inn%d" % t for t in range(RD)])
+SEMAPHORES = (["cv", "cs", "cp", "cg", "lsd", "lst", "lth", "ltb", "lown", "lpair", "loc", "early", "late", "outw", "arrw", "innw", "outi", "arri", "outj", "arrj", "inni", "lsh", "lfill", "lbig"]
+              + ["out0", "arr0"] + [a + str(t) + p for a in ("out", "arr") for t in range(1, RD) for p in "01"] + ["inn%d" % t for t in range(RD)])
 
 
 def rank_program(g, core, T, topo):
@@ -163,24 +160,28 @@ def rank_program(g, core, T, topo):
     WALL = WO + ["remin%d" % j for j in range(N - 1)] + ["mine", "remfill"]
     OSD = ["osd0", "osd1"]
     BO = ["b0", "b1", "b2", "b3"]
-    FILL = ["fill%d" % j for j in range(N)]
+    CUT = CFG["cut"]
+    FILL = ["fill%d" % j for j in range(6)]
     BALL = FILL + ["bin%d" % j for j in range(N)] + ["sec%d" % j for j in range(N)]
+    BALL += ["bin%d_%d" % (p, j) for p in range(2) for j in range(N)]
     later = []
     TO = ["tw0", "tw1", "tw2", "tw3"]
     TW = TO + ["twfill", "twmine"] + ["twin%d" % j for j in range(N - 1)]
     dests = [(r + 1 + j) % N for j in range(N - 1)]
-    own_win = T.win[:, 0:1024]
+    own_win = T.big[:, 0:1024]
+    SN = 2048
+    ident = T.idp[:, 15:143]
 
     def send(t):
         for w in CFG["pick"].split():
             q, a, b = w[0], int(w[1:].split("-")[0]), int(w[1:].split("-")[-1])
             if "-" in w:
-                gather(q, T.snd[:, 896 * t + 16 * a:896 * t + 16 * b], own_win, T.osd[:, a:b], WO + OSD, units("s%d_" % t, a, b))
+                gather(q, T.big[:, SN + 16 * a:SN + 16 * b], own_win, T.osd[:, a:b], WO + OSD, units("s%d_" % t, a, b))
             else:
-                dma(q, "out%d" % t, T.outd[7 * t + a], T.snd[15::16, 896 * t + 128 * a:896 * t + 128 * a + 128],
+                dma(q, "out%d" % t, T.outd[7 * t + a], T.big[15::16, SN + 128 * a:SN + 128 * a + 128],
                     units("s%d_" % t, 8 * a, 8 * a + 8), ["od%d_%d" % (t, a)])
         remote("0", lambda j: T.outd[j], T.land[r])
-        gather("s", T.win[:, 1024 + 128 * r:1152 + 128 * r], own_win, T.osd[:, 56:64], WO + OSD + ["remfill"], ["mine"])
+        gather("s", T.big[:, 1024 + 128 * r:1152 + 128 * r], own_win, T.osd[:, 56:64], WO + OSD + ["remfill"], ["mine"])
 
     def remote(n, src, dst):
         need("g", [("out" + n, None)])
@@ -197,69 +198,79 @@ def rank_program(g, core, T, topo):
     def span(t):
         return 4096 * (1 - t % 2)
 
-    def share(n, k, src, rd):
-        if CFG["bygroup"]:
-            dma(CFG["oq"], "out" + n, T.land3[64 * k + r:64 * k + 64:8], src, rd, ["od" + n])
-            need("g", [("out" + n, None)])
-            ids = [DstId(rid=a, pnc=b) for a, b in [topo.addr(T.cores[d], core) for d in dests]]
-            engines = topo.engines(core, T.cores[dests[0]])
-            g.remote_dma_fused([RemoteDMATransfer(dst_ids=ids, dma_engine_mask=1 << engines[c], remote_sem=T.sem["arr" + n],
-                                                  srcs=[T.land3[64 * k + 8 * c + r]], dsts=[T.land3[64 * k + 8 * c + r]] * (N - 1))
-                                for c in range(8)], local_sem=T.sem.loc)
-            cnt["loc"] = cnt.get("loc", 0) + 8
-            cnt["arr" + n] = 8 * (N - 1)
-        else:
-            dma(CFG["oq"], "out" + n, T.land2[8 * k + r], src, rd, ["od" + n])
-            remote(n, lambda j: T.land2[8 * k + r], T.land2[8 * k + r])
-
-    def take(n, k, a, wr):
-        lastw["land" + n] = ("arr" + n, cnt["arr" + n])
-        if CFG["bygroup"]:
-            dma("y", "inn" + n, T.big[15::16, a:a + 4096], T.land3[64 * k:64 * k + 64], ["land" + n, "od" + n] + FILL, [wr + "0"])
-        else:
-            for j, q in enumerate([r] + dests):
-                dma("y" if j <= CFG["ny"] or n == "i" else "s", "inn" + n, T.big[15::16, a + 512 * q:a + 512 * q + 512], T.land2[8 * k + q],
-                    ["land" + n if j else "od" + n, FILL[(a + 512 * q) // 1024]], [wr + str(j)])
+    def share(n, land, k, src, rd, q, m=1):
+        w = 64 // m
+        if q:
+            dma(q, "out" + n, land[w * k + r:w * k + w:8], src, rd, ["od" + n])
+        need("g", [("out" + n, None)])
+        ids = [DstId(rid=a, pnc=b) for a, b in [topo.addr(T.cores[d], core) for d in dests]]
+        engines = topo.engines(core, T.cores[dests[0]])
+        g.remote_dma_fused([RemoteDMATransfer(dst_ids=ids[j::m], dma_engine_mask=1 << engines[m * c + j], remote_sem=T.sem["arr" + n],
+                                              srcs=[land[w * k + 8 * c + r]], dsts=[land[w * k + 8 * c + r]] * len(ids[j::m]))
+                            for c in range(8 // m) for j in range(m)], local_sem=T.sem.loc)
+        cnt["loc"] = cnt.get("loc", 0) + 8
+        cnt["arr" + n] = 8 // m * (N - 1)
 
     def receive(t):
         if t:
-            return take(str(t), t - 1, span(t), "bin")
+            for p, m in enumerate(CFG["m"]):
+                n, a, w = "%d%d" % (t, p), span(t) + 2048 * p, 64 // m
+                lastw["land" + n] = ("arr" + n, cnt["arr" + n])
+                for j in range(m):
+                    dma("s" if t == RD - 1 and p and j % 2 else "y", "inn%d" % t, T.big[15 + 16 * j::16 * m, a:a + 2048],
+                        T["part%d" % p][w * (t - 1):w * t, 128 // m * j:128 // m * (j + 1), :],
+                        ["land" + n, "od" + n] + filled(a, a + 2048),
+                        ["bin%d_%d" % (p, j)] + ([] if t > 1 or j else units("s0_", 0, 56) + ["sws"] if p else WALL))
+            return
         lastw["land0"] = ("arr0", N - 1)
         for j, q in enumerate(dests):
-            dma("y" if j < CFG["ny"] else "s", "inn0", T.win[15::16, 1024 + 128 * q:1024 + 128 * q + 128], T.land[q], ["land0", "remfill"], ["remin%d" % j])
+            dma("y" if j < CFG["ny"] else "s", "inn0", T.big[15::16, 1024 + 128 * q:1024 + 128 * q + 128], T.land[q], ["land0", "remfill"], ["remin%d" % j])
 
     def fill(j, q):
-        out = T.big[:, 1024 * j:1024 * j + 1024]
+        a, b = CUT[j], CUT[j + 1]
+        if a == b:
+            return
+        out = T.big[:, a:b]
         if q == "g":
-            op("g", lambda: g.iota(out, [[0, 1024]], 0, 0, allow_small_or_imprecise_dtypes=True), [], ["fill%d" % j])
+            op("g", lambda: g.iota(out, [[0, b - a]], 0, 0, allow_small_or_imprecise_dtypes=True), [], [FILL[j]])
         elif q == "v":
-            op("v", lambda: V.memset(out, 0.0), [], ["fill%d" % j])
+            op("v", lambda: V.memset(out, 0.0), [], [FILL[j]])
         else:
-            dma("y", "lfill", out, T.owns[:], ["owns"], ["fill%d" % j])
+            dma("y", "lfill", out, T.raw[:, 0:(b - a) // 16, :], ["raw0"], [FILL[j]])
+
+    def filled(a, b):
+        return [FILL[j] for j in range(6) if CUT[j] < b and a < CUT[j + 1]]
 
     def compose(h):
-        for src, off, name, out, bank in ((T.zz, T.oth, "z", T.bth, "pc0"), (T.ww, T.onb, "u", T.bnb, "pb1")):
-            for q, a, b in (("v", 0, CFG["cc"]), ("s", CFG["cc"], 96)):
-                gather(q, src[:, 16 * a:16 * b], T.tw[:, 0:2048], off[:, h, a:b], TW + LI["oth"] + LI["onb"], units(name, a, b))
-            mms([(T[bank][:, 0:96], T.sel2[:, 15 - i:143 - i], src[:, i:1536:16], i == 0, i == 15) for i in range(16)],
-                units(name, 0, 96) + ["sel2"], [bank])
-            if name == "z":
-                later.append(lambda: copy("v", T.bth[:, h, :], T.pc0[:, 0:96], [], ["pc0", "bth%d" % h]))
-            else:
-                later.pop()()
-                later.append(lambda: copy("v", T.bnb[:, h, :], T.pb1[:, 0:96], [], ["pb1", "bnb%d" % h]))
+        def offsets(out, name, c, bank):
+            return lambda: copy("v", out[:, h, c:c + 48], T[bank][:, 0:48], [], [bank] + units(name + str(h) + "_", c, c + 48))
+        jobs = [(T.zz, 0, "z", T.bth, "bth", 0, "pc0"), (T.ww, 2, "u", T.bnb, "bnb", 0, "pc1"),
+                (T.zz, 0, "z", T.bth, "bth", 48, "pb0"), (T.ww, 2, "u", T.bnb, "bnb", 48, "pb1")]
+        for src, off, name, out, oname, c, bank in jobs:
+            for q, a, b in (("v", c, c + CFG["cc"]), ("s", c + CFG["cc"], c + 48)):
+                gather(q, src[:, 16 * a:16 * b], T.tw[:, 0:2048], T.olist[:, off + h, a:b], TW + LI["oth"] + LI["onb"], units(name, a, b))
+            mms([(T[bank][:, 0:48], T.sel2[:, 15 - i:143 - i], src[:, 16 * c + i:16 * c + 768:16], i == 0, i == 15) for i in range(16)],
+                units(name, c, c + 48) + ["sel2"], [bank])
+            if h and bank == CFG["sat"]:
+                copy("v", T.shb[:], T.shst[:], ["shst0%d" % c for c in range(8)] + ["shst1"], ["shb"])
+                for p in range(2):
+                    a = 4096 + 2048 * p
+                    dma("y", "inni", T.big[15::16, a:a + 2048], T.shb[:, 128 * p:128 * p + 128], ["shb"] + filled(a, a + 2048), ["sec%d" % p])
+            if len(later) == 2:
+                later.pop(0)()
+            later.append(offsets(out, oname, c, bank))
+        later.pop(0)()
 
-    dma("y", "lst", T.stst[:], T.st[:], [], ["stst"])
-    dma("s", "lsd", T.sdst[:], T.sd[:], [], ["sdst"])
-    dma("s", "lsh", T.shst[:], T.st[:, 512:1024], [], ["shst"])
-    n1 = CFG["n1"]
-    dma("y", "lpair", T.raw[:, 0:n1, :], T.pair[:, 0:16 * n1], [], ["raw0"])
+    dma("s", "lst", T.stst[:], T.st[:], [], ["stst"])
     op("g", lambda: g.iota(T.dif[:], [[-1, 144]], 15, 1, allow_small_or_imprecise_dtypes=True), [], ["dif"])
     op("g", lambda: g.iota(T.mi[:, 0:1], [[0, 1]], 0, 1), [], ["mi0"])
     op("g", lambda: g.iota(T.low[:], [[1, 256]], 0, 0, allow_small_or_imprecise_dtypes=True), [], ["low"])
+    share("i", T.landi, 0, T.st[:, 512:768], [], "y", 4)
+    dma("y", "lsd", T.sdst[:], T.sd[:], [], ["sdst"])
+    dma("y", "lpair", T.raw[:], T.pair[:], [], ["raw0"])
     op("g", lambda: g.iota(T.desc[:], [[0, 16], [-1, 16]], 15, 0, allow_small_or_imprecise_dtypes=True), [], ["desc"])
-    op("v", lambda: V.memset(T.win[:, 1024:2048], 0.0), [], ["remfill"])
-    copy("s", T.tw[:, 1024:2048], T.win[:, 1024:2048], ["remfill"], ["twfill"])
+    op("v", lambda: V.memset(T.big[:, 1024:2048], 0.0), [], ["remfill"])
+    copy("s", T.tw[:, 1024:2048], T.big[:, 1024:2048], ["remfill"], ["twfill"])
     op("v", lambda: V.tensor_scalar(T.idp[:], T.dif[:], 0.0, None, A.is_equal), ["dif"], ["idp"])
     op("v", lambda: V.tensor_scalar(T.mi[:, 1:2], T.mi[:, 0:1], 8, None, A.bitwise_and), ["mi0"], ["mi1"])
     op("v", lambda: V.memset(T.sel[:], 0.0), [], ["sel"])
@@ -268,17 +279,13 @@ def rank_program(g, core, T, topo):
     op("v", lambda: V.memset(T.sel2[:], 0.0), [], ["sel2"])
     op("v", lambda: V.memset(T.mn[:, 7:8], 0.0), [], ["mn0"])
     op("v", lambda: V.tensor_scalar(T.sel[:, 15:128:16], T.dif[:, 30:143:16], 0.0, None, A.is_equal), ["dif"], ["sel"])
-    for j in range(2):
-        op("v", lambda: V.tensor_scalar(T.mk[:, 2 + 2 * j:4 + 2 * j], T.low[:, 0:2], 2.0 * r + 16 * j, T.mk[:, 1:2], A.add, A.mult),
-           ["low", "mk1"], ["mk2%d" % j])
+    op("v", lambda: V.tensor_scalar(T.mk[:, 2:6], T.low[:, r:r + 25:8], T.mk[:, 1:2], None, A.mult), ["low", "mk1"], ["mk2"])
 
     def numbers(j):
         op("v", lambda: V.tensor_scalar(T.tw[:, 256 * j:256 * j + 256], T.low[:], T.mk[:, 0:1], T.mk[:, 2 + j:3 + j], A.mult, A.add),
-           ["low", "mk0", "mk20", "mk21"], ["tw%d" % j])
+           ["low", "mk0", "mk2"], ["tw%d" % j])
     copy("v", T.stb[:], T.stst[:], ["stst"], ["stb"])
-    copy("v", T.shb[:], T.shst[:], ["shst"], ["shb"])
-    share("i", 3, T.shb[:], ["shb"])
-    dma("y", "lpair", T.raw[:, n1:256, :], T.pair[:, 16 * n1:4096], [], ["raw1"])
+    fill(0, "g")
     k = 8 * (N - 1 - r)
     if k:
         copy("v", T.osd[:, 0:k], T.sdst[:, 64 - k:64], ["sdst"], ["osd0"])
@@ -289,28 +296,26 @@ def rank_program(g, core, T, topo):
         j0, bank = b * CFG["n0"], T["pe%d" % b]
         mms([(bank[:, 64 * j:64 * j + 64], T.idp[:, j0 + j:j0 + j + 128], T.stb[:], True, True) for j in range(n)],
             ["stb", "idp"], ["pe%d" % (2 * b), "pe%d" % (2 * b + 1)])
-        copy(q, T.win[:, 64 * j0:64 * (j0 + n)], bank[:, 0:64 * n], [], ["pe%d" % (2 * b), "pe%d" % (2 * b + 1)] + WO[2 * b:2 * b + 2])
+        copy(q, T.big[:, 64 * j0:64 * (j0 + n)], bank[:, 0:64 * n], [], ["pe%d" % (2 * b), "pe%d" % (2 * b + 1)] + WO[2 * b:2 * b + 2])
     send(0)
 
+    dma("y", "outj", T.land3[64 + r:128:8], T.st[:, 768:1024], [], ["odj"])
     dma("y", "ltb", T.tbst[:], T.tb[:], [], ["tbst"])
-    dma("y", "lth", T.thst[:], T.th[:], [], ["thst"])
-    dma("y", "lth", T.nbst[:], T.nb[:], [], ["nbst"])
+    dma("y", "lth", T.lists[:, 0:6], T.th[:], [], ["thst"])
+    dma("y", "lth", T.lists[:, 6:12], T.nb[:], [], ["nbst"])
     if CFG["ownearly"]:
         dma("y", "lown", T.owns[:], T.own[:], [], ["owns"])
     numbers(2)
     numbers(3)
-    gather("s", T.snd[:, 896:1792], T.tw[:, 0:1024], T.osd[:, 0:56], TO + OSD, ["sws"])
+    gather("s", T.big[:, SN + 896:SN + 1792], T.tw[:, 0:1024], T.osd[:, 0:56], TO + OSD, ["sws"])
     for j in range(N - 1):
-        dma(CFG["wq"][j], "outw", T.outw[j], T.snd[7::8, 896 + 128 * j:1024 + 128 * j], ["sws"], ["ow%d" % j])
-    if "g" not in CFG["ps"]:
-        fill(7, "g")
-        remote("w", lambda j: T.outw[j], T.landw[r])
-    op("v", lambda: V.tensor_scalar(T.idb[:], T.dif[:, 15:143], 0.0, None, A.is_equal), ["dif"], ["idb"])
-    op("v", lambda: V.tensor_scalar(T.idf[:], T.dif[:, 15:143], 0.0, None, A.is_equal), ["dif"], ["idf"])
+        dma(CFG["wq"][j], "outw", T.outw[j], T.big[7::8, SN + 896 + 128 * j:SN + 1024 + 128 * j], ["sws"], ["ow%d" % j])
+    fill(4, "g")
     op("v", lambda: V.tensor_scalar(T.rst[:], T.desc[:], 15.0, 2.0 ** 90, A.is_equal, A.mult), ["desc"], ["rst"])
     op("v", lambda: V.tensor_scalar(T.sel2[:, 15:128:16], T.dif[:, 30:143:16], -8.0, 256.0, A.is_equal, A.mult), ["dif"], ["sel2"])
     op("v", lambda: V.tensor_tensor(T.sel2[:, 15:128:16], T.sel2[:, 15:128:16], T.sel[:, 15:128:16], A.add), ["sel"], ["sel2"])
-    PX = []
+    fill(1, "v")
+    PX, behind = [], []
     a = 0
     while a < NP:
         t0 = 37 * a % 256
@@ -318,31 +323,41 @@ def rank_program(g, core, T, topo):
         q = CFG["ps"][len(PX) % len(CFG["ps"])]
         PX.append("px%d" % a)
         o, i = T.px[:, 16 * a:16 * (a + n)], T.raw[:, t0:t0 + 37 * (n - 1) + 1:37, :]
-        if q == "g":
-            op("g", lambda: g.affine_select(o, i, [[0, 16 * n]], A.is_ge, 0.0, 0, 0), ["raw0", "raw1"], PX[-1:])
+        if q == "l":
+            behind.append((o, i, PX[-1:]))
         else:
             copy(q, o, i, ["raw0", "raw1"], PX[-1:])
         a += n
-    if "g" in CFG["ps"]:
-        remote("w", lambda j: T.outw[j], T.landw[r])
-        fill(7, "g")
     op("v", lambda: V.tensor_scalar(T.tbm[:], T.tbst[:], 173, None, A.mult), ["tbst"], ["tbm"])
     for q in range(4):
-        copy("v", T.oth[:, :, 24 * q:24 * q + 24], T.thst[:, :, q, :], ["thst"], ["oth%d" % q])
-    op("v", lambda: V.tensor_scalar(T.tba[:], T.tbm[:], 255, None, A.bitwise_and), ["tbm"], ["tba"])
-    for q in range(4):
-        copy("v", T.onb[:, :, 24 * q:24 * q + 24], T.nbst[:, :, q, :], ["nbst"], ["onb%d" % q])
+        copy("v", T.olist[:, :, 24 * q:24 * q + 24], T.lists[:, :, q, :], ["thst", "nbst"], ["oth%d" % q, "onb%d" % q])
+        if q == 0:
+            op("v", lambda: V.tensor_scalar(T.tba[:], T.tbm[:], 255, None, A.bitwise_and), ["tbm"], ["tba"])
     for q in range(4):
         op("v", lambda: V.tensor_scalar(T.tb16[:, :, 24 * q:24 * q + 24], T.tba[:, :, q, :], 16.0, None, A.mult), ["tba"], ["tb16%d" % q])
     LI = {n: [n + str(q) for q in range(4)] for n in ("oth", "onb", "tb16")}
 
     def places():
+        if CFG["wlate"]:
+            need("g", [("inn0", None)])
+        remote("w", lambda j: T.outw[j], T.landw[r])
+        share("j", T.land3, 1, None, [], None)
+        lastw["landi"] = ("arri", cnt["arri"])
+        lastw["landj"] = ("arrj", cnt["arrj"])
         lastw["landw"] = ("arrw", N - 1)
+        fill(3, "g")
+        if CFG["f1"] == 0:
+            fill(2, "y")
+        for c in range(8):
+            dma("y", "lsh", T.shst[16 * c:16 * c + 16, 0:128], T.landi[8 * (c // 4):8 * (c // 4) + 8, 32 * (c % 4):32 * (c % 4) + 32, :],
+                ["landi", "odi"], ["shst0%d" % c])
+        if CFG["f1"] == 1:
+            fill(2, "y")
         for j, q in enumerate(dests):
             dma("y", "innw", T.tw[7::8, 1024 + 128 * q:1152 + 128 * q], T.landw[q], ["landw", "twfill"], ["twin%d" % j])
-        for j in range(N - 2, -1, -1):
-            if CFG["fq"][j] != "v":
-                fill(j, CFG["fq"][j])
+        if CFG["f1"] == 2:
+            fill(2, "y")
+        dma("y", "lsh", T.shst[:, 128:256], T.land3[64:128], ["landj", "odj"], ["shst1"])
 
     def pe(a, b):
         return T["pe%d" % (a // 2)][:, 384 + 128 * (a % 2):384 + 128 * (a % 2 + b - a)]
@@ -360,20 +375,20 @@ def rank_program(g, core, T, topo):
             op("p", lambda: P.transpose(T[bank][0:m, 128:256], T.mn[:, 23 + 128 * a:8 + 128 * b:16], T.idf[:]),
                ["mn%d" % c for c in range(a, b)] + ["idf"], [bank])
             copy(q, T.eo[0:m, o:o + 128], T[bank][0:m, 128:256], [], [bank, "eo%d" % o])
-            for c in range(a, b):
+            for c in range(a, a + len(dq)):
                 dma(dq[c - a], sem, T.e[:, w0 + 128 * c:w0 + 128 * c + 128], T.eo[8 * (c - a):8 * (c - a) + 8, o:o + 128], ["eo%d" % o], [])
 
         def step(w):
             kind, q = w[0], w[1] if w[1] in "vs" else "v"
-            nums = [int(x) for x in w.lstrip("ZUWCXELFKYPBTvs").split("-")]
+            nums = [int(x) for x in w.lstrip("ZUWCXELFKYPBTOvs").split("-")]
             a, b = nums[0], nums[-1]
             if later and kind == CFG["pop"]:
                 later.pop()()
             if kind == "Z":
                 if t:
-                    gather(q, T.zz[:, 16 * a:16 * b], T.big[:, 0:1024 * N], T.bth[:, h, a:b], BALL + ["bth%d" % h], units("z", a, b), 16.0)
+                    gather(q, T.zz[:, 16 * a:16 * b], T.big[:, 0:1024 * N], T.bth[:, h, a:b], BALL + units("bth%d_" % h, a, b), units("z", a, b), 16.0)
                 else:
-                    gather(q, T.zz[:, 16 * a:16 * b], T.win[:, 0:2048], T.oth[:, h, a:b], WALL + LI["oth"], units("z", a, b), 16.0)
+                    gather(q, T.zz[:, 16 * a:16 * b], T.big[:, 0:2048], T.olist[:, h, a:b], WALL + LI["oth"], units("z", a, b), 16.0)
             elif kind == "W":
                 bank = blocks[a]
                 mms([(T[bank][:, 0:b - a], T.sel[:, 15 - i:143 - i], T.ww[:, 16 * a + i:16 * b:16], False, i == 15) for i in range(16)],
@@ -384,13 +399,14 @@ def rank_program(g, core, T, topo):
             elif kind == "X":
                 gather(q, T.xx[:, 16 * a:16 * b], T.px[:, 0:16 * NP], T.col[:, a:b], PX + units("c", a, b), units("x", a, b))
             elif kind == "E":
-                mms([(pe(a, a + 1), T.xx[:, 384 * a + 128 * e:384 * a + 128 * e + 128], T.idb[:], False, e == 2) for e in range(3)],
-                    units("x", 24 * a, 24 * a + 24) + ["idb"], ["pe%d" % a])
+                mms([(pe(a, a + 1), T.xx[:, 384 * a + 128 * e:384 * a + 128 * e + 128], ident, False, e == 2) for e in range(3)],
+                    units("x", 24 * a, 24 * a + 24) + ["idp"], ["pe%d" % a])
             elif kind == "L":
                 op("v", lambda: V.tensor_tensor_scan(T.mn[:, 8 + 128 * a:8 + 128 * b], T.rst[:, 0:128 * (b - a)], pe(a, b), 0.0, A.add, A.min),
                    ["rst"], chunks("pe", a, b) + chunks("mn", a, b))
-                if last and b % 2 == 0:
-                    energies_out(b - 2, b, "pc%d" % (a // 2), "s", "ys", "late")
+            elif kind == "O":
+                if last:
+                    energies_out(a, b, "pc%d" % (a // 2), q, CFG["eq"][a:b], "late")
             elif kind == "F":
                 op("v", lambda: V.tensor_tensor(T.nlt[:, 128 * a:128 * b], pe(a, b), T.mn[:, 7 + 128 * a:7 + 128 * b], A.is_ge),
                    chunks("mn", max(a - 1, 0), b), chunks("pe", a, b) + chunks("nlt", a, b))
@@ -399,60 +415,65 @@ def rank_program(g, core, T, topo):
                    chunks("nlt", a, b) + ["desc"], chunks("arg", a, b))
             elif kind == "Y":
                 if t:
-                    gather(q, T.ww[:, 16 * a:16 * b], T.big[:, 0:1024 * N], T.bnb[:, h, a:b], BALL + ["bnb%d" % h], units("u", a, b))
+                    gather(q, T.ww[:, 16 * a:16 * b], T.big[:, 0:1024 * N], T.bnb[:, h, a:b], BALL + units("bnb%d_" % h, a, b), units("u", a, b))
                 else:
-                    gather(q, T.ww[:, 16 * a:16 * b], T.win[:, 0:2048], T.onb[:, h, a:b], WALL + LI["onb"], units("u", a, b))
+                    gather(q, T.ww[:, 16 * a:16 * b], T.big[:, 0:2048], T.olist[:, 2 + h, a:b], WALL + LI["onb"], units("u", a, b))
             elif kind == "P":
                 bank = blocks[a]
                 mms([(T[bank][:, 0:b - a], T.sel[:, 15 - i:143 - i], T.zz[:, 16 * a + i:16 * b:16], False, False) for i in range(16)],
                     units("z", a, b) + ["sel"], [bank])
             elif kind == "B":
                 bank = ["pb0", "pb0", "pb1", "pb0"][a]
-                mms([(T[bank][:, 128 * a:128 * a + 128], T.arg[:, 128 * a:128 * a + 128], T.idb[:], True, True)], ["arg%d" % a, "idb"], [bank])
+                mms([(T[bank][:, 128 * a:128 * a + 128], T.arg[:, 128 * a:128 * a + 128], ident, True, True)], ["arg%d" % a, "idp"], [bank])
             elif kind == "T":
                 bank = ["pb0", "pb0", "pb1", "pb0"][a]
                 c0, c1 = w0 + 128 * a, w0 + 128 * b
                 if last:
                     flip(q, T.yo[:, c0:c1], T[bank][:, 128 * a:128 * b], [], [bank, "yo%d" % a])
-                    dma("s" if q == "s" else "y", "late", T.y[:, c0:c1], T.yo[15::16, c0:c1], ["yo%d" % a], [])
+                    dma(CFG["yq"][a], "late", T.y[:, c0:c1], T.yo[15::16, c0:c1], ["yo%d" % a], [])
                 else:
                     flip(q, T.new[:, 512 * t + 128 * a:512 * t + 128 * b], T[bank][:, 128 * a:128 * b], [], [bank] + BO[a:b])
+                    if b % 2 == 0:
+                        p = b // 2 - 1
+                        n, src = "%d%d" % (t + 1, p), T.new[15::16, 512 * t + 256 * p:512 * t + 256 * p + 256]
+                        share(n, T["part%d" % p], t, src, BO[2 * p:2 * p + 2], "y", CFG["m"][p])
 
         order = (last and CFG["last"] or CFG["order"]).split()
         for j, w in enumerate([w for w in order if w[0] == "W"]):
             a, b = [int(x) for x in w[1:].split("-")]
             blocks[a] = ["pc0", "pc1", "pb1"][j]
-            mms([(T[blocks[a]][:, 0:b - a], T.idb[:], T.tb16[:, h, a:b], True, False)], ["idb"] + LI["tb16"], [blocks[a]])
+            mms([(T[blocks[a]][:, 0:b - a], ident, T.tb16[:, h, a:b], True, False)], ["idp"] + LI["tb16"], [blocks[a]])
 
         def alone():
             for q in range(4):
-                mms([(pe(q, q + 1), T.owns[:, w0 + 128 * q:w0 + 128 * q + 128], T.idb[:], True, False)], ["owns", "idb"], ["pe%d" % q])
-        if t:
+                mms([(pe(q, q + 1), T.owns[:, w0 + 128 * q:w0 + 128 * q + 128], ident, True, False)], ["owns", "idp"], ["pe%d" % q])
+        if t or CFG["ownearly"]:
             alone()
         receive(t)
+        if last:
+            dma("y", "early", T.y[:, 0:512], T.yo[15::16, 0:512], ["yoe"], [])
+            for c in range(4):
+                dma("y", "early", T.e[:, 128 * c:128 * c + 128], T.eo[8 * c:8 * c + 8, 0:128], ["eo0"], [])
         if t == 0:
+            for o, i, name in behind:
+                copy("s", o, i, ["raw0", "raw1"], name)
             need("y", [("inn0", None)])
             if not CFG["ownearly"]:
                 dma("y", "lown", T.owns[:], T.own[:], [], ["owns"])
             places()
         for w in order:
-            if t == 0 and w == "E0":
+            if t == 0 and w == CFG["aat"] and not CFG["ownearly"]:
                 alone()
             step(w)
         if not last:
-            share(str(t + 1), t, T.new[15::16, 512 * t:512 * t + 512], BO)
             if t == 0:
-                for j in range(N):
-                    if CFG["fq"][j] == "v":
-                        fill(j, "v")
-                take("i", 3, 4096, "sec")
                 gather("s", T.tw[:, 1024 + 128 * r:1152 + 128 * r], T.tw[:, 0:1024], T.osd[:, 56:64], TO + OSD + ["twfill"], ["twmine"])
             if t < 2:
                 compose(1 - t)
             if t == RD - 2:
+                op("v", lambda: V.tensor_scalar(T.idf[:], T.dif[:, 15:143], 0.0, None, A.is_equal), ["dif"], ["idf"])
                 copy("v", T.yo[:, 0:512], T.new[:, 512 * t:512 * t + 512], BO, ["yoe"])
-                dma("y", "early", T.y[:, 0:512], T.yo[15::16, 0:512], ["yoe"], [])
-                energies_out(0, 4, "pb1", "v", "yyyy", "early")
+                energies_out(0, 4, "pb1", "v", "", "early")
 
     for sem in [s for s in cnt if s != "late"] + ["late"]:
         if known["g"].get(sem, 0) < cnt[sem]:

from concourse.bass import DstId, RemoteDMATransfer
from concourse.mybir import AluOpType, ActivationFunctionType

N, RD = 8, 4
NP = 256 + 15
CFG = dict(ny=4, oq="y", ownearly=0, cc=24, f1=1, sat="pc1", cut=[3840, 4480, 4480, 5504, 6912, 8192, 8192], m=[4, 2], hq=["yyyy", "yyyy"], wlate=1, n0=9, last="", pick="v0-16 s40-56 y0 y1 y5 v16-28 s28-40 y2 y3 s4 s6", ps="vsvvlvvv", pop="Y", yq="yysy", eq="yyyy", aat="E0", bygroup=1, wq="yyyyyyy", fq="eeyyyggg", order="""
    Zv0-24 Zs24-48 P0-48 Yv0-24 Ys24-48 W0-48 Zv48-74 Zs74-96 P48-96 C0-48 Yv48-66 Ys66-96 W48-96
    Xv0-24 Xs24-48 C48-96 E0 E1 Xv48-58 Xs58-72 E2 Xs72-96 L0-2 Os0-2 E3 F0-2 L2-3 K0-2 B0 B1 F2-3 Ts0-2
    L3-4 Os2-4 K2-3 B2 F3-4 Ts2-3 K3-4 B3 Tv3-4""")

SCRATCH = {
    "stst": ("sbuf", [128, 64], "int32"),
    "stb": ("sbuf", [128, 64], "bfloat16"),
    "idp": ("sbuf", [128, 144], "bfloat16"),
    "sdst": ("sbuf", [128, 64], "int32"),
    "lists": ("sbuf", [128, 12, 4, 8], "int32"),
    "olist": ("sbuf", [128, 4, 96], "uint16"),
    "tbst": ("sbuf", [128, 192], "int32"),
    "tbm": ("sbuf", [128, 192], "int32"),
    "tba": ("sbuf", [128, 6, 4, 8], "int32"),
    "osd": ("sbuf", [128, 64], "uint16"),
    "tb16": ("sbuf", [128, 2, 96], "bfloat16"),
    "col": ("sbuf", [128, 96], "uint16"),
    "big": ("sbuf", [128, 1024 * N], "bfloat16"),
    "tw": ("sbuf", [128, 2048], "bfloat16"),
    "low": ("sbuf", [128, 256], "bfloat16"),
    "mk": ("sbuf", [128, 8], "float32"),
    "mi": ("sbuf", [128, 2], "int32"),
    "sel2": ("sbuf", [128, 144], "bfloat16"),
    "bth": ("sbuf", [128, 2, 96], "uint16"),
    "bnb": ("sbuf", [128, 2, 96], "uint16"),
    "outw": ("dram", [7, 128, 16], "bfloat16"),
    "landw": ("dram", [8, 128, 16], "bfloat16"),
    "land3": ("dram", [128, 128, 2], "int32"),
    "landi": ("dram", [16, 128, 8], "int32"),
    "part0": ("dram", [192 // CFG["m"][0], 128, 2 * CFG["m"][0]], "bfloat16"),
    "part1": ("dram", [192 // CFG["m"][1], 128, 2 * CFG["m"][1]], "bfloat16"),
    "new": ("sbuf", [128, 512 * 3], "bfloat16"),
    "shst": ("sbuf", [128, 256], "int32"),
    "shb": ("sbuf", [128, 256], "bfloat16"),
    "owns": ("sbuf", [128, 1024], "bfloat16"),
    "raw": ("sbuf", [128, 256, 16], "bfloat16"),
    "px": ("sbuf", [128, NP * 16], "bfloat16"),
    "zz": ("sbuf", [128, 1536], "bfloat16"),
    "ww": ("sbuf", [128, 1536], "bfloat16"),
    "xx": ("sbuf", [128, 1536], "bfloat16"),
    "dif": ("sbuf", [128, 144], "float32"),
    "idf": ("sbuf", [128, 128], "float32"),
    "sel": ("sbuf", [128, 144], "bfloat16"),
    "desc": ("sbuf", [128, 256], "bfloat16"),
    "rst": ("sbuf", [128, 256], "bfloat16"),
    "mn": ("sbuf", [128, 520], "float32"),
    "nlt": ("sbuf", [128, 512], "bfloat16"),
    "arg": ("sbuf", [128, 512], "bfloat16"),
    "yo": ("sbuf", [128, 1024], "float32"),
    "eo": ("sbuf", [128, 384], "float32"),
    "outd": ("dram", [7, 128, 8], "bfloat16"),
    "land": ("dram", [8, 128, 8], "bfloat16"),
}
for _k in ("pe0", "pe1"):
    SCRATCH[_k] = ("psum", [128, 1024], "float32")
for _k in ("pc0", "pc1", "pb0", "pb1"):
    SCRATCH[_k] = ("psum", [128, 512], "float32")

SEMAPHORES = (["cv", "cs", "cp", "cg", "lsd", "lst", "lth", "ltb", "lown", "lpair", "loc", "early", "late", "outw", "arrw", "innw", "outi", "arri", "outj", "arrj", "inni", "lsh", "lfill", "lbig"]
              + ["out0", "arr0"] + [a + str(t) + p for a in ("out", "arr") for t in range(1, RD) for p in "01"] + ["inn%d" % t for t in range(RD)])


def rank_program(g, core, T, topo):
    r = T.rank_of(core)
    if r is None:
        return
    A, F = AluOpType, ActivationFunctionType
    V, S, P = g.vector, g.scalar, g.tensor
    Q = {"g": g, "v": V, "s": S, "p": P, "y": g.sync}
    known = {q: {} for q in Q}
    cnt, clock, lastw, readers = {}, {}, {}, {}

    def fix(ev):
        return ev if ev[1] is not None else (ev[0], cnt[ev[0]])

    def clk(ev):
        return clock.get(ev) or clock.get((ev[0], None)) or {}

    def need(q, evs):
        evs = sorted(set(fix(e) for e in evs))
        for e in evs:
            if known[q].get(e[0], 0) >= e[1]:
                continue
            if any(o != e and (clk(o).get(e[0], 0) >= e[1] or (o[0] == e[0] and o[1] > e[1])) for o in evs):
                continue
            Q[q].wait_ge(T.sem[e[0]], e[1])
            known[q][e[0]] = e[1]
            for k, n in clk(e).items():
                known[q][k] = max(known[q].get(k, 0), n)

    def deps(q, rd, wr):
        d = [lastw[x] for x in list(rd) + list(wr) if x in lastw]
        for x in wr:
            d += readers.get(x, [])
        return [e for e in d if not (q == "p" and e[0] == "cp")]

    def note(ev, rd, wr):
        for x in rd:
            readers.setdefault(x, []).append(ev)
        for x in wr:
            lastw[x] = ev
            readers[x] = []

    def op(q, fn, rd, wr):
        need(q, deps(q, rd, wr))
        sem = "c" + q
        fn().then_inc(T.sem[sem], 1)
        cnt[sem] = cnt.get(sem, 0) + 1
        ev = (sem, cnt[sem])
        clock[ev] = dict(known[q])
        note(ev, rd, wr)

    def dma(q, sem, out, in_, rd, wr):
        need(q, deps(q, rd, wr))
        Q[q].dma_start(out, in_).then_inc(T.sem[sem], 16)
        cnt[sem] = cnt.get(sem, 0) + 16
        c = clock.setdefault((sem, None), {})
        for k, n in known[q].items():
            c[k] = max(c.get(k, 0), n)
        note((sem, None), rd, wr)

    def gather(q, out, win, off, rd, wr, scale=None):
        if q == "s":
            op(q, lambda: S.activation(out, win.indirect(off), F.Copy, scale=scale or 1.0), rd, wr)
        elif scale:
            op(q, lambda: V.tensor_scalar(out, win.indirect(off), scale, None, A.mult), rd, wr)
        else:
            op(q, lambda: V.tensor_copy(out, win.indirect(off)), rd, wr)

    def flip(q, out, in_, rd, wr):
        if q == "v":
            op(q, lambda: V.tensor_scalar(out, in_, -1.0, 15.0, A.mult, A.add), rd, wr)
        else:
            op(q, lambda: S.activation(out, in_, F.Copy, bias=15.0, scale=-1.0), rd, wr)

    def copy(q, out, in_, rd, wr):
        if q == "v":
            op(q, lambda: V.tensor_copy(out, in_), rd, wr)
        else:
            op(q, lambda: S.activation(out, in_, F.Copy), rd, wr)

    def mms(items, rd, wr):
        def fn():
            last = None
            for it in items:
                last = P.matmul(*it)
            return last
        op("p", fn, rd, wr)

    def units(name, a, b):
        return ["%s%d" % (name, k) for k in range(a // 2, b // 2)]

    WO = ["w0", "w1", "w2", "w3"]
    WALL = WO + ["remin%d" % j for j in range(N - 1)] + ["mine", "remfill"]
    OSD = ["osd0", "osd1"]
    BO = ["b0", "b1", "b2", "b3"]
    CUT = CFG["cut"]
    FILL = ["fill%d" % j for j in range(6)]
    BALL = FILL + ["bin%d" % j for j in range(N)] + ["sec%d" % j for j in range(N)]
    BALL += ["bin%d_%d" % (p, j) for p in range(2) for j in range(N)]
    later = []
    TO = ["tw0", "tw1", "tw2", "tw3"]
    TW = TO + ["twfill", "twmine"] + ["twin%d" % j for j in range(N - 1)]
    dests = [(r + 1 + j) % N for j in range(N - 1)]
    own_win = T.big[:, 0:1024]
    SN = 2048
    ident = T.idp[:, 15:143]

    def send(t):
        for w in CFG["pick"].split():
            q, a, b = w[0], int(w[1:].split("-")[0]), int(w[1:].split("-")[-1])
            if "-" in w:
                gather(q, T.big[:, SN + 16 * a:SN + 16 * b], own_win, T.osd[:, a:b], WO + OSD, units("s%d_" % t, a, b))
            else:
                dma(q, "out%d" % t, T.outd[7 * t + a], T.big[15::16, SN + 128 * a:SN + 128 * a + 128],
                    units("s%d_" % t, 8 * a, 8 * a + 8), ["od%d_%d" % (t, a)])
        remote("0", lambda j: T.outd[j], T.land[r])
        gather("s", T.big[:, 1024 + 128 * r:1152 + 128 * r], own_win, T.osd[:, 56:64], WO + OSD + ["remfill"], ["mine"])

    def remote(n, src, dst):
        need("g", [("out" + n, None)])
        trs = []
        for j, d in enumerate(dests):
            c = T.cores[d]
            rid, pid = topo.addr(c, core)
            trs.append(RemoteDMATransfer(dst_ids=[DstId(rid=rid, pnc=pid)], dma_engine_mask=1 << topo.engines(core, c)[j],
                                         remote_sem=T.sem["arr" + n], src=src(j), dst=dst))
        g.remote_dma_fused(trs, local_sem=T.sem.loc)
        cnt["loc"] = cnt.get("loc", 0) + N - 1
        cnt["arr" + n] = N - 1

    def span(t):
        return 4096 * (1 - t % 2)

    def share(n, land, k, src, rd, q, m=1):
        w = 64 // m
        if q:
            dma(q, "out" + n, land[w * k + r:w * k + w:8], src, rd, ["od" + n])
        need("g", [("out" + n, None)])
        ids = [DstId(rid=a, pnc=b) for a, b in [topo.addr(T.cores[d], core) for d in dests]]
        engines = topo.engines(core, T.cores[dests[0]])
        g.remote_dma_fused([RemoteDMATransfer(dst_ids=ids[j::m], dma_engine_mask=1 << engines[m * c + j], remote_sem=T.sem["arr" + n],
                                              srcs=[land[w * k + 8 * c + r]], dsts=[land[w * k + 8 * c + r]] * len(ids[j::m]))
                            for c in range(8 // m) for j in range(m)], local_sem=T.sem.loc)
        cnt["loc"] = cnt.get("loc", 0) + 8
        cnt["arr" + n] = 8 // m * (N - 1)

    def receive(t):
        if t:
            for p, m in enumerate(CFG["m"]):
                n, a, w = "%d%d" % (t, p), span(t) + 2048 * p, 64 // m
                lastw["land" + n] = ("arr" + n, cnt["arr" + n])
                for j in range(m):
                    dma("s" if t == RD - 1 and p and j % 2 else "y", "inn%d" % t, T.big[15 + 16 * j::16 * m, a:a + 2048],
                        T["part%d" % p][w * (t - 1):w * t, 128 // m * j:128 // m * (j + 1), :],
                        ["land" + n, "od" + n] + filled(a, a + 2048),
                        ["bin%d_%d" % (p, j)] + ([] if t > 1 or j else units("s0_", 0, 56) + ["sws"] if p else WALL))
            return
        lastw["land0"] = ("arr0", N - 1)
        for j, q in enumerate(dests):
            dma("y" if j < CFG["ny"] else "s", "inn0", T.big[15::16, 1024 + 128 * q:1024 + 128 * q + 128], T.land[q], ["land0", "remfill"], ["remin%d" % j])

    def fill(j, q):
        a, b = CUT[j], CUT[j + 1]
        if a == b:
            return
        out = T.big[:, a:b]
        if q == "g":
            op("g", lambda: g.iota(out, [[0, b - a]], 0, 0, allow_small_or_imprecise_dtypes=True), [], [FILL[j]])
        elif q == "v":
            op("v", lambda: V.memset(out, 0.0), [], [FILL[j]])
        else:
            dma("y", "lfill", out, T.raw[:, 0:(b - a) // 16, :], ["raw0"], [FILL[j]])

    def filled(a, b):
        return [FILL[j] for j in range(6) if CUT[j] < b and a < CUT[j + 1]]

    def compose(h):
        def offsets(out, name, c, bank):
            return lambda: copy("v", out[:, h, c:c + 48], T[bank][:, 0:48], [], [bank] + units(name + str(h) + "_", c, c + 48))
        jobs = [(T.zz, 0, "z", T.bth, "bth", 0, "pc0"), (T.ww, 2, "u", T.bnb, "bnb", 0, "pc1"),
                (T.zz, 0, "z", T.bth, "bth", 48, "pb0"), (T.ww, 2, "u", T.bnb, "bnb", 48, "pb1")]
        for src, off, name, out, oname, c, bank in jobs:
            for q, a, b in (("v", c, c + CFG["cc"]), ("s", c + CFG["cc"], c + 48)):
                gather(q, src[:, 16 * a:16 * b], T.tw[:, 0:2048], T.olist[:, off + h, a:b], TW + LI["oth"] + LI["onb"], units(name, a, b))
            mms([(T[bank][:, 0:48], T.sel2[:, 15 - i:143 - i], src[:, 16 * c + i:16 * c + 768:16], i == 0, i == 15) for i in range(16)],
                units(name, c, c + 48) + ["sel2"], [bank])
            if h and bank == CFG["sat"]:
                copy("v", T.shb[:], T.shst[:], ["shst0%d" % c for c in range(8)] + ["shst1"], ["shb"])
                for p in range(2):
                    a = 4096 + 2048 * p
                    dma("y", "inni", T.big[15::16, a:a + 2048], T.shb[:, 128 * p:128 * p + 128], ["shb"] + filled(a, a + 2048), ["sec%d" % p])
            if len(later) == 2:
                later.pop(0)()
            later.append(offsets(out, oname, c, bank))
        later.pop(0)()

    dma("s", "lst", T.stst[:], T.st[:], [], ["stst"])
    op("g", lambda: g.iota(T.dif[:], [[-1, 144]], 15, 1, allow_small_or_imprecise_dtypes=True), [], ["dif"])
    op("g", lambda: g.iota(T.mi[:, 0:1], [[0, 1]], 0, 1), [], ["mi0"])
    op("g", lambda: g.iota(T.low[:], [[1, 256]], 0, 0, allow_small_or_imprecise_dtypes=True), [], ["low"])
    share("i", T.landi, 0, T.st[:, 512:768], [], "y", 4)
    dma("y", "lsd", T.sdst[:], T.sd[:], [], ["sdst"])
    dma("y", "lpair", T.raw[:], T.pair[:], [], ["raw0"])
    op("g", lambda: g.iota(T.desc[:], [[0, 16], [-1, 16]], 15, 0, allow_small_or_imprecise_dtypes=True), [], ["desc"])
    op("v", lambda: V.memset(T.big[:, 1024:2048], 0.0), [], ["remfill"])
    copy("s", T.tw[:, 1024:2048], T.big[:, 1024:2048], ["remfill"], ["twfill"])
    op("v", lambda: V.tensor_scalar(T.idp[:], T.dif[:], 0.0, None, A.is_equal), ["dif"], ["idp"])
    op("v", lambda: V.tensor_scalar(T.mi[:, 1:2], T.mi[:, 0:1], 8, None, A.bitwise_and), ["mi0"], ["mi1"])
    op("v", lambda: V.memset(T.sel[:], 0.0), [], ["sel"])
    op("v", lambda: V.tensor_scalar(T.mk[:, 0:1], T.mi[:, 1:2], 0.125, None, A.mult), ["mi1"], ["mk0"])
    op("v", lambda: V.tensor_scalar(T.mk[:, 1:2], T.mi[:, 1:2], -0.125, 1.0, A.mult, A.add), ["mi1"], ["mk1"])
    op("v", lambda: V.memset(T.sel2[:], 0.0), [], ["sel2"])
    op("v", lambda: V.memset(T.mn[:, 7:8], 0.0), [], ["mn0"])
    op("v", lambda: V.tensor_scalar(T.sel[:, 15:128:16], T.dif[:, 30:143:16], 0.0, None, A.is_equal), ["dif"], ["sel"])
    op("v", lambda: V.tensor_scalar(T.mk[:, 2:6], T.low[:, r:r + 25:8], T.mk[:, 1:2], None, A.mult), ["low", "mk1"], ["mk2"])

    def numbers(j):
        op("v", lambda: V.tensor_scalar(T.tw[:, 256 * j:256 * j + 256], T.low[:], T.mk[:, 0:1], T.mk[:, 2 + j:3 + j], A.mult, A.add),
           ["low", "mk0", "mk2"], ["tw%d" % j])
    copy("v", T.stb[:], T.stst[:], ["stst"], ["stb"])
    fill(0, "g")
    k = 8 * (N - 1 - r)
    if k:
        copy("v", T.osd[:, 0:k], T.sdst[:, 64 - k:64], ["sdst"], ["osd0"])
    copy("v", T.osd[:, k:64], T.sdst[:, 0:64 - k], ["sdst"], ["osd1"])
    numbers(0)
    numbers(1)
    for b, (q, n) in enumerate((("s", CFG["n0"]), ("v", 16 - CFG["n0"]))):
        j0, bank = b * CFG["n0"], T["pe%d" % b]
        mms([(bank[:, 64 * j:64 * j + 64], T.idp[:, j0 + j:j0 + j + 128], T.stb[:], True, True) for j in range(n)],
            ["stb", "idp"], ["pe%d" % (2 * b), "pe%d" % (2 * b + 1)])
        copy(q, T.big[:, 64 * j0:64 * (j0 + n)], bank[:, 0:64 * n], [], ["pe%d" % (2 * b), "pe%d" % (2 * b + 1)] + WO[2 * b:2 * b + 2])
    send(0)

    dma("y", "outj", T.land3[64 + r:128:8], T.st[:, 768:1024], [], ["odj"])
    dma("y", "ltb", T.tbst[:], T.tb[:], [], ["tbst"])
    dma("y", "lth", T.lists[:, 0:6], T.th[:], [], ["thst"])
    dma("y", "lth", T.lists[:, 6:12], T.nb[:], [], ["nbst"])
    if CFG["ownearly"]:
        dma("y", "lown", T.owns[:], T.own[:], [], ["owns"])
    numbers(2)
    numbers(3)
    gather("s", T.big[:, SN + 896:SN + 1792], T.tw[:, 0:1024], T.osd[:, 0:56], TO + OSD, ["sws"])
    for j in range(N - 1):
        dma(CFG["wq"][j], "outw", T.outw[j], T.big[7::8, SN + 896 + 128 * j:SN + 1024 + 128 * j], ["sws"], ["ow%d" % j])
    fill(4, "g")
    op("v", lambda: V.tensor_scalar(T.rst[:], T.desc[:], 15.0, 2.0 ** 90, A.is_equal, A.mult), ["desc"], ["rst"])
    op("v", lambda: V.tensor_scalar(T.sel2[:, 15:128:16], T.dif[:, 30:143:16], -8.0, 256.0, A.is_equal, A.mult), ["dif"], ["sel2"])
    op("v", lambda: V.tensor_tensor(T.sel2[:, 15:128:16], T.sel2[:, 15:128:16], T.sel[:, 15:128:16], A.add), ["sel"], ["sel2"])
    fill(1, "v")
    PX, behind = [], []
    a = 0
    while a < NP:
        t0 = 37 * a % 256
        n = min((255 - t0) // 37 + 1, NP - a)
        q = CFG["ps"][len(PX) % len(CFG["ps"])]
        PX.append("px%d" % a)
        o, i = T.px[:, 16 * a:16 * (a + n)], T.raw[:, t0:t0 + 37 * (n - 1) + 1:37, :]
        if q == "l":
            behind.append((o, i, PX[-1:]))
        else:
            copy(q, o, i, ["raw0", "raw1"], PX[-1:])
        a += n
    op("v", lambda: V.tensor_scalar(T.tbm[:], T.tbst[:], 173, None, A.mult), ["tbst"], ["tbm"])
    for q in range(4):
        copy("v", T.olist[:, :, 24 * q:24 * q + 24], T.lists[:, :, q, :], ["thst", "nbst"], ["oth%d" % q, "onb%d" % q])
        if q == 0:
            op("v", lambda: V.tensor_scalar(T.tba[:], T.tbm[:], 255, None, A.bitwise_and), ["tbm"], ["tba"])
    for q in range(4):
        op("v", lambda: V.tensor_scalar(T.tb16[:, :, 24 * q:24 * q + 24], T.tba[:, :, q, :], 16.0, None, A.mult), ["tba"], ["tb16%d" % q])
    LI = {n: [n + str(q) for q in range(4)] for n in ("oth", "onb", "tb16")}

    def places():
        if CFG["wlate"]:
            need("g", [("inn0", None)])
        remote("w", lambda j: T.outw[j], T.landw[r])
        share("j", T.land3, 1, None, [], None)
        lastw["landi"] = ("arri", cnt["arri"])
        lastw["landj"] = ("arrj", cnt["arrj"])
        lastw["landw"] = ("arrw", N - 1)
        fill(3, "g")
        if CFG["f1"] == 0:
            fill(2, "y")
        for c in range(8):
            dma("y", "lsh", T.shst[16 * c:16 * c + 16, 0:128], T.landi[8 * (c // 4):8 * (c // 4) + 8, 32 * (c % 4):32 * (c % 4) + 32, :],
                ["landi", "odi"], ["shst0%d" % c])
        if CFG["f1"] == 1:
            fill(2, "y")
        for j, q in enumerate(dests):
            dma("y", "innw", T.tw[7::8, 1024 + 128 * q:1152 + 128 * q], T.landw[q], ["landw", "twfill"], ["twin%d" % j])
        if CFG["f1"] == 2:
            fill(2, "y")
        dma("y", "lsh", T.shst[:, 128:256], T.land3[64:128], ["landj", "odj"], ["shst1"])

    def pe(a, b):
        return T["pe%d" % (a // 2)][:, 384 + 128 * (a % 2):384 + 128 * (a % 2 + b - a)]

    def chunks(name, a, b):
        return [name + str(c) for c in range(a, b)]

    for t in range(RD):
        h, last = t & 1, t == RD - 1
        w0 = 512 * h
        blocks = {}

        def energies_out(a, b, bank, q, dq, sem):
            m, o = 8 * (b - a), 0 if sem == "early" else 128 + 64 * a
            op("p", lambda: P.transpose(T[bank][0:m, 128:256], T.mn[:, 23 + 128 * a:8 + 128 * b:16], T.idf[:]),
               ["mn%d" % c for c in range(a, b)] + ["idf"], [bank])
            copy(q, T.eo[0:m, o:o + 128], T[bank][0:m, 128:256], [], [bank, "eo%d" % o])
            for c in range(a, a + len(dq)):
                dma(dq[c - a], sem, T.e[:, w0 + 128 * c:w0 + 128 * c + 128], T.eo[8 * (c - a):8 * (c - a) + 8, o:o + 128], ["eo%d" % o], [])

        def step(w):
            kind, q = w[0], w[1] if w[1] in "vs" else "v"
            nums = [int(x) for x in w.lstrip("ZUWCXELFKYPBTOvs").split("-")]
            a, b = nums[0], nums[-1]
            if later and kind == CFG["pop"]:
                later.pop()()
            if kind == "Z":
                if t:
                    gather(q, T.zz[:, 16 * a:16 * b], T.big[:, 0:1024 * N], T.bth[:, h, a:b], BALL + units("bth%d_" % h, a, b), units("z", a, b), 16.0)
                else:
                    gather(q, T.zz[:, 16 * a:16 * b], T.big[:, 0:2048], T.olist[:, h, a:b], WALL + LI["oth"], units("z", a, b), 16.0)
            elif kind == "W":
                bank = blocks[a]
                mms([(T[bank][:, 0:b - a], T.sel[:, 15 - i:143 - i], T.ww[:, 16 * a + i:16 * b:16], False, i == 15) for i in range(16)],
                    units("u", a, b) + ["sel"], [bank])
            elif kind == "C":
                bank = blocks[a]
                copy("v", T.col[:, a:b], T[bank][:, 0:b - a], [], [bank] + units("c", a, b))
            elif kind == "X":
                gather(q, T.xx[:, 16 * a:16 * b], T.px[:, 0:16 * NP], T.col[:, a:b], PX + units("c", a, b), units("x", a, b))
            elif kind == "E":
                mms([(pe(a, a + 1), T.xx[:, 384 * a + 128 * e:384 * a + 128 * e + 128], ident, False, e == 2) for e in range(3)],
                    units("x", 24 * a, 24 * a + 24) + ["idp"], ["pe%d" % a])
            elif kind == "L":
                op("v", lambda: V.tensor_tensor_scan(T.mn[:, 8 + 128 * a:8 + 128 * b], T.rst[:, 0:128 * (b - a)], pe(a, b), 0.0, A.add, A.min),
                   ["rst"], chunks("pe", a, b) + chunks("mn", a, b))
            elif kind == "O":
                if last:
                    energies_out(a, b, "pc%d" % (a // 2), q, CFG["eq"][a:b], "late")
            elif kind == "F":
                op("v", lambda: V.tensor_tensor(T.nlt[:, 128 * a:128 * b], pe(a, b), T.mn[:, 7 + 128 * a:7 + 128 * b], A.is_ge),
                   chunks("mn", max(a - 1, 0), b), chunks("pe", a, b) + chunks("nlt", a, b))
            elif kind == "K":
                op("v", lambda: V.tensor_tensor_scan(T.arg[:, 128 * a:128 * b], T.nlt[:, 128 * a:128 * b], T.desc[:, 0:128 * (b - a)], 0.0, A.mult, A.max),
                   chunks("nlt", a, b) + ["desc"], chunks("arg", a, b))
            elif kind == "Y":
                if t:
                    gather(q, T.ww[:, 16 * a:16 * b], T.big[:, 0:1024 * N], T.bnb[:, h, a:b], BALL + units("bnb%d_" % h, a, b), units("u", a, b))
                else:
                    gather(q, T.ww[:, 16 * a:16 * b], T.big[:, 0:2048], T.olist[:, 2 + h, a:b], WALL + LI["onb"], units("u", a, b))
            elif kind == "P":
                bank = blocks[a]
                mms([(T[bank][:, 0:b - a], T.sel[:, 15 - i:143 - i], T.zz[:, 16 * a + i:16 * b:16], False, False) for i in range(16)],
                    units("z", a, b) + ["sel"], [bank])
            elif kind == "B":
                bank = ["pb0", "pb0", "pb1", "pb0"][a]
                mms([(T[bank][:, 128 * a:128 * a + 128], T.arg[:, 128 * a:128 * a + 128], ident, True, True)], ["arg%d" % a, "idp"], [bank])
            elif kind == "T":
                bank = ["pb0", "pb0", "pb1", "pb0"][a]
                c0, c1 = w0 + 128 * a, w0 + 128 * b
                if last:
                    flip(q, T.yo[:, c0:c1], T[bank][:, 128 * a:128 * b], [], [bank, "yo%d" % a])
                    dma(CFG["yq"][a], "late", T.y[:, c0:c1], T.yo[15::16, c0:c1], ["yo%d" % a], [])
                else:
                    flip(q, T.new[:, 512 * t + 128 * a:512 * t + 128 * b], T[bank][:, 128 * a:128 * b], [], [bank] + BO[a:b])
                    if b % 2 == 0:
                        p = b // 2 - 1
                        n, src = "%d%d" % (t + 1, p), T.new[15::16, 512 * t + 256 * p:512 * t + 256 * p + 256]
                        share(n, T["part%d" % p], t, src, BO[2 * p:2 * p + 2], "y", CFG["m"][p])

        order = (last and CFG["last"] or CFG["order"]).split()
        for j, w in enumerate([w for w in order if w[0] == "W"]):
            a, b = [int(x) for x in w[1:].split("-")]
            blocks[a] = ["pc0", "pc1", "pb1"][j]
            mms([(T[blocks[a]][:, 0:b - a], ident, T.tb16[:, h, a:b], True, False)], ["idp"] + LI["tb16"], [blocks[a]])

        def alone():
            for q in range(4):
                mms([(pe(q, q + 1), T.owns[:, w0 + 128 * q:w0 + 128 * q + 128], ident, True, False)], ["owns", "idp"], ["pe%d" % q])
        if t or CFG["ownearly"]:
            alone()
        receive(t)
        if last:
            dma("y", "early", T.y[:, 0:512], T.yo[15::16, 0:512], ["yoe"], [])
            for c in range(4):
                dma("y", "early", T.e[:, 128 * c:128 * c + 128], T.eo[8 * c:8 * c + 8, 0:128], ["eo0"], [])
        if t == 0:
            for o, i, name in behind:
                copy("s", o, i, ["raw0", "raw1"], name)
            need("y", [("inn0", None)])
            if not CFG["ownearly"]:
                dma("y", "lown", T.owns[:], T.own[:], [], ["owns"])
            places()
        for w in order:
            if t == 0 and w == CFG["aat"] and not CFG["ownearly"]:
                alone()
            step(w)
        if not last:
            if t == 0:
                gather("s", T.tw[:, 1024 + 128 * r:1152 + 128 * r], T.tw[:, 0:1024], T.osd[:, 56:64], TO + OSD + ["twfill"], ["twmine"])
            if t < 2:
                compose(1 - t)
            if t == RD - 2:
                op("v", lambda: V.tensor_scalar(T.idf[:], T.dif[:, 15:143], 0.0, None, A.is_equal), ["dif"], ["idf"])
                copy("v", T.yo[:, 0:512], T.new[:, 512 * t:512 * t + 512], BO, ["yoe"])
                energies_out(0, 4, "pb1", "v", "", "early")

    for sem in [s for s in cnt if s != "late"] + ["late"]:
        if known["g"].get(sem, 0) < cnt[sem]:
            g.wait_ge(T.sem[sem], cnt[sem])
